import numpy as np, ml_dtypes
CORES = [35,38,43,46]
N = 4
BF = ml_dtypes.bfloat16
def gentries(a):
    return np.ascontiguousarray(a.reshape(8, 16, -1).transpose(0, 2, 1)).reshape(8, -1)
def gtable(e):
    e = np.asarray(e); return np.ascontiguousarray(e.reshape(8, -1, 16).transpose(0, 2, 1)).reshape(128, -1).astype(np.int32)
V, L, D, T, RO = 4096, 256, 8, 2, 8
def rows_of(rng, a, b):
    u = np.concatenate([a, b]); w = np.concatenate([b, a])
    return w[np.argsort(u + 0.5 * rng.random(u.size))].reshape(V, D)
def graph(rng, kind):
    i = np.arange(V)
    if kind == 2:
        m = i.reshape(-1, 2, D); a = np.repeat(m[:, 0], D, axis=1).reshape(-1); b = np.tile(m[:, 1], (1, D)).reshape(-1)
    elif kind == 1:
        s = 1 + rng.permutation(V - 1)[:D]; w = i[:, None] ^ s; keep = w > i[:, None]
        a = np.repeat(i[:, None], D, axis=1)[keep]; b = w[keep]
    else:
        s = 1 + rng.permutation(V // 2 - 1)[:D // 2]; a = np.repeat(i, D // 2); b = ((i[:, None] + s) & (V - 1)).reshape(-1)
        turn = rng.random(a.size) < 0.5; a, b = np.where(turn, b, a), np.where(turn, a, b)
        o = rng.permutation(a.size); k = a.size // 2; p, q = o[:k], o[k:2 * k]
        def key(u, w): return np.minimum(u, w) * V + np.maximum(u, w)
        new = np.concatenate([key(a[p], b[q]), key(a[q], b[p])])
        z, inv, cnt = np.unique(new, return_inverse=True, return_counts=True)
        no = np.isin(new, key(a, b)) | (cnt[inv.reshape(-1)] > 1); no = no[:k] | no[k:] | (a[p] == b[q]) | (a[q] == b[p])
        p, q = p[~no], q[~no]; bp, bq = b[p].copy(), b[q].copy(); b[p] = bq; b[q] = bp
    m = rng.permutation(V)
    return rows_of(rng, m[a], m[b])
def graphs(rng, kinds):
    return np.stack([np.stack([graph(rng, int(kinds[r, g])) for g in range(8)]) for r in range(N)])
def parts(rng):
    return (rng.integers(-15, 16, (N, 8, 16, V)), rng.integers(-15, 16, (N, 8, 16, L)), rng.integers(-15, 16, (N, 8, 16, L)), rng.integers(-255, 256, (N, 8, 16, 1)),
            rng.integers(0, V, (N, 8, L)), rng.integers(0, D + T, (N, 8, L)))
def pack(nbs, x, c, y, h, v, j):
    def bf(a): return np.ascontiguousarray(a.reshape(N, 128, -1)).astype(np.float32).astype(BF)
    return {"adj": np.ascontiguousarray(nbs.transpose(0, 1, 3, 2).reshape(N, 8 * D, V)).astype(np.int32), "x": bf(x), "c0": bf(c), "y0": bf(y), "h": bf(h),
            "v0": np.stack([gtable(a) for a in v]), "j0": np.stack([gtable(a) for a in j])}
def setup_inputs(rng):
    return pack(graphs(rng, rng.choice(np.array([0, 0, 0, 1]), (N, 8))), *parts(rng))
def setup_inputs_ties(rng):
    x, c, y, h, v, j = parts(rng); pool = rng.integers(-1, 2, (N, 8, 16, 6))
    x = np.take_along_axis(pool, np.broadcast_to(rng.integers(0, 6, (N, 8, 1, V)), (N, 8, 16, V)), 3)
    c = rng.integers(-1, 2, c.shape) * (rng.random((N, 8, 1, L)) < 0.9)
    y = rng.integers(-1, 2, y.shape)
    return pack(graphs(rng, rng.choice(np.array([0, 1, 2]), (N, 8))), x, c, y, h, v, j)
def setup_inputs_tops(rng):
    x, c, y, h, v, j = parts(rng); k = L // 2
    c[..., :k] = 0; j[..., :k] = rng.integers(D, D + T, (N, 8, k))
    h[:, :4, 0] = -1; h[:, 0, 1:6] = 128; h[:, 1, 1:6] = -128; h[:, 4:6] = 255; h[:, 6:] = -255
    y[..., 0:3] = 0; y[:, :, 0, 1] = 1; y[:, :, 0, 2] = 2; y[..., 3] = 15; y[..., 4] = -15
    y[..., 5:k:2] = np.abs(y[..., 5:k:2])
    for i in range(4):
        y[:, :2, :, 5 + i] = 0
        y[:, :2, 1:6, 5 + i] = (1, -1, 1, -1)[i] * np.clip((1, 1, 2, 2)[i] * V // 128 - 15 * np.arange(5), 0, 15)
    v[..., 9:13] = (np.add.reduce(h * y, axis=2) & (V - 1))[..., 9:13]
    nbs = graphs(rng, rng.choice(np.array([0, 1]), (N, 8)))
    for r in range(N):
        for g in range(8):
            n = int(rng.integers(0, V)); q = int(rng.integers(0, D)); w = int(nbs[r, g, n, q])
            x[r, g, :, n] = 15; x[r, g, :, w] = -15
            v[r, g, k:k + 4] = n; j[r, g, k:k + 4] = np.array([q, q, D, D]); c[r, g, :, k:k + 4] = np.array([15, -15, 15, -15])
            m = int(rng.choice(np.setdiff1d(np.arange(V), np.concatenate([np.array([n, w]), nbs[r, g, n], nbs[r, g, w]]))))
            t = rng.integers(2, 6, D); t[0] = 5; t[1] = 6; t[D - 1] = 1
            x[r, g][:, nbs[r, g, m]] = 15 - (np.argsort(rng.random((16, D)), axis=0) < t)
            p, z = ((3, 1), (10, 2))[g % 2]; x[r, g, :, m] = 15 - z * (rng.permutation(16) < p)
            v[r, g, k + 4:k + 8] = m; j[r, g, k + 4:k + 8] = np.array([D, D, 0, 0]); c[r, g, :, k + 4:k + 8] = np.array([15, -15, 15, -15])
    return pack(nbs, x, c, y, h, v, j)
def setup_inputs_deep(rng):
    x, c, y, h, v, j = parts(rng); i = np.arange(V); q = i * 3390 // V
    col = np.concatenate([(q[None, :] // 15 + np.arange(15)[:, None]) // 15, (q % 15)[None, :]])
    w = (i[:, None] + np.concatenate([np.arange(-(D // 2), 0), np.arange(1, D // 2 + 1)])) & (V - 1)
    nbs = np.zeros((N, 8, V, D), np.int64); way = np.array([15] * 15 + [1])
    for r in range(N):
        for g in range(8):
            m = rng.permutation(V); u = (w, w[:, ::-1], rng.permuted(w, axis=1), rng.permuted(w, axis=1))[g % 4]
            nbs[r, g, m] = m[u]; x[r, g][:, m] = col
            c[r, g] = way[:, None] * np.where(rng.random(L) < 0.7, 1, -1)
    return pack(nbs, x, c, y, h, v, j)
def setup_inputs_alike(rng):
    x, c, y, h, v, j = parts(rng)
    v[:, 0::4] = rng.integers(0, V, (N, 2, 1)); v[:, 1::4] = rng.choice(np.array([0, V - 1]), (N, 2, L))
    j[:, 0::4] = np.arange(L) % (D + T); c[:, 2] = c[:, 2, :, :1]
    j[:, 3::3] = rng.integers(D, D + T, (N, 2, L)); c[:, 6] = 0; j[:, 5] = 0
    for r in range(N):
        n = int(rng.integers(0, V)); x[r, 7, :, n] = 15; v[r, 7] = n
    c[:, 7] = 15; j[:, 7] = rng.integers(0, D, (N, L))
    kinds = np.tile(np.array([2, 0, 2, 1, 0, 2, 1, 2]), (N, 1))
    return pack(graphs(rng, kinds), x, c, y, h, v, j)
def setup_inputs_spread(rng):
    x, c, y, h, v, j = parts(rng)
    def size(a, top): return np.sign(a) * ((np.abs(a) * np.exp2(-top * rng.random(a.shape[:2] + (1, a.shape[3])))).astype(np.int64))
    x = size(x, 5) * (rng.random((N, 8, 1, V)) > 0.0625); c = size(c, 4); y = size(y, 4); h = size(h, 7)
    v = (V * rng.random((N, 8, L)) ** 4).astype(np.int64)
    return pack(graphs(rng, rng.choice(np.array([0, 0, 1]), (N, 8))), x, c, y, h, np.minimum(v, V - 1), j)
def check_inputs(d):
    bad = []
    for k, lo, hi in (("adj", 0, V - 1), ("x", -15, 15), ("c0", -15, 15), ("y0", -15, 15), ("h", -255, 255), ("v0", 0, V - 1), ("j0", 0, D + T - 1)):
        a = np.asarray(d[k]).astype(np.float32)
        if not (np.min(a) >= lo and np.max(a) <= hi and np.all(a == np.floor(a))): bad.append("range of " + k)
    me = np.arange(V)[:, None]; own = twice = oneway = False
    for a in np.asarray(d["adj"]).astype(np.int64).reshape(N * 8, D, V):
        w = np.ascontiguousarray(a.T); s = np.sort(w, axis=1)
        own = own or bool(np.any(w == me)); twice = twice or bool(np.any(s[:, 1:] == s[:, :-1]))
        oneway = oneway or bool(np.any(np.sort((me * V + w).reshape(-1)) != np.sort((w * V + me).reshape(-1))))
    if own: bad.append("adj: a node is its own neighbour")
    if twice: bad.append("adj: a neighbour stands twice at one node")
    if oneway: bad.append("adj: an edge goes one way only")
    return bad
def reference(adj, x, c0, y0, h, v0, j0):
    P = N * 8
    nbs = np.ascontiguousarray(adj.reshape(P, D, V).transpose(0, 2, 1)).astype(np.int64)
    def turned(a): return np.ascontiguousarray(a.astype(np.float32).reshape(P, 16, -1).transpose(0, 2, 1)).astype(np.int32)
    xs, c, y, hs = turned(x), turned(c0), turned(y0), turned(h)
    v = np.stack([gentries(a) for a in v0]).reshape(P, L).astype(np.int64); j = np.stack([gentries(a) for a in j0]).reshape(P, L).astype(np.int64)
    b = np.arange(P)[:, None]; b3 = b[:, :, None]
    def parent(e, c):
        near = nbs[b, e]
        s = np.einsum("pldi,pli->pld", xs[b3, near], c); mine = np.einsum("pli,pli->pl", xs[b, e], c)
        best = np.argmax(s, axis=2)[:, :, None]
        return np.where(np.take_along_axis(s, best, 2)[:, :, 0] > mine, np.take_along_axis(near, best, 2)[:, :, 0], e)
    for step in range(1, RO + 1):
        back = j >= D; nv = v; nj = j + T; found = np.zeros((P, L), bool); fv = v
        for t in range(T):
            ok = ~back & (j + t < D)
            w = np.where(ok, nbs[b, v, np.minimum(j + t, D - 1)], v)
            f = parent(w, c)
            if t == 0: fv = f
            hit = ok & ~found & (f == v)
            nv = np.where(hit, w, nv); nj = np.where(hit, 0, nj); found = found | hit
        at = np.argmax(nbs[b, fv] == v[:, :, None], axis=2)
        again = np.add.reduce(hs.astype(np.int64) * y, axis=2) & (V - 1)
        up = back & (fv != v); top = back & (fv == v)
        v = np.where(up, fv, np.where(top, again, nv)); j = np.where(up, 1 + at, np.where(top, 0, nj))
        if step % 2 == 0:
            xv = xs[b, v]
            y = np.roll(xv.reshape(N, 8, L, 16), 1, axis=0).reshape(P, L, 16)
            c = np.clip(c + np.sign(y - xv), -15, 15)
    return {"vo": v.reshape(N, 8, L).astype(np.float32), "jo": j.reshape(N, 8, L).astype(np.float32),
            "co": np.ascontiguousarray(c.transpose(0, 2, 1)).reshape(N, 128, L).astype(np.float32)}

@@ -1,0 +1,519 @@
+import numpy as np
+from concourse.mybir import AluOpType as I, ActivationFunctionType as F
+
+V, STEPS, LANES = 4096, 8, 256
+HALF = 2048.0
+NB = 2
+W = LANES // NB
+ML = W // 16
+KK = W // 8
+CH = 32
+NCH = W // CH
+IW = V + 8
+NCHG = STEPS // 2
+WCH = 4
+
+SCRATCH = {}
+SIZE = {}
+def _d(where, dtype, **cols):
+    for n in cols:
+        SCRATCH[n] = (where, [128, cols[n]], dtype)
+def _b(dtype, **cols):
+    for n in cols:
+        SIZE[n] = cols[n]
+        SCRATCH[n] = ("sbuf", [128, NB * cols[n]], dtype)
+_d("sbuf", "int32", win=V, v0i=16, j0i=16, ip=1, ti=8)
+_d("sbuf", "float32", wf=V, iw=IW, cf=16, r128=128, re0=128, re1=128, iv0=128, iv1=128, mi=128, rg8=8, pc=8, mk=8, mk8=8)
+_d("sbuf", "bfloat16", xw=V, hs=1, ow=24, jp=24, hp=24, jwc=128, bc=1024, bce=2048, r0b=128, zb=128, idb=128, kc=16 * KK)
+_d("sbuf", "float16", v0f=16, j0f=16, ep0=24, ep1=24, pm0=128, pm1=128, vi0=128, vi1=128)
+_b("float32", uc=W, av=W, zz=W, bb=W, bq=W, ta=8 * KK, tb=8 * KK, tc=4 * KK, te=2 * KK, ok=2 * KK, dd=2 * KK, gt=2 * KK, gk=2 * KK,
+   hh=2 * KK, hd=2 * KK, bk=KK, j2=KK, jq=KK, vk=KK, ag=KK, up=KK, tp=KK, at=KK, ba=KK, pu=KK, sa=KK, ho=KK,
+   dy=W, sg=W, cn=W, co_s=W, vo_s=W, jo_s=W)
+_b("float16", pr1=W, pr2=W, eh=2 * KK, vv=2 * KK, us=KK, nu=KK)
+_b("bfloat16", c0s=W, y0s=W, eq=W, po=2 * W, xg=16 * W, cc=2 * W, cd=16 * W, rb=2 * KK, jb=KK)
+_b("int32", t3=2 * KK, ri=2 * KK, ai=KK, aj=KK)
+_b("uint16", lv=ML, lu=ML, le=2 * ML, lb=W)
+for _k in range(NB):
+    for _n in ("PS", "PC", "PH", "PL"):
+        SCRATCH["%s_%d" % (_n, _k)] = ("psum", [128, 512], "float32")
+    for _t in range(NCHG):
+        for _n in ("xv%d", "yv%d"):
+            SIZE[_n % _t] = W
+            SCRATCH[_n % _t + "_%d" % _k] = ("sbuf", [128, W], "bfloat16")
+
+LOADS = ["d_%d" % k for k in range(6 + 2 * WCH + 3 * NB)]
+SEMAPHORES = ["sV", "sA", "sP", "sG", "sent"] + LOADS + ["ar_%d_%d" % (b, t) for b in range(NB) for t in range(NCHG)]
+
+CYC, PCYC, GAMMA, WAKE = 0.00083, 0.00042, 1.5, 0.08
+
+
+def engines_of(topo, src, dst):
+    return topo.engines(src, dst)[:8]
+
+
+def build(T, topo, core):
+    rank, n_ranks = T.rank_of(core), len(T.cores)
+    nxt, prv = T.cores[(rank + 1) % n_ranks], T.cores[(rank - 1) % n_ranks]
+    ops, last_w, readers, bank = [], {}, {}, {}
+    now = [0]
+
+    def op(eng, cost, reads, writes, fns, sem=None, val=0, lat=0.0, alt=None):
+        deps, soft = set(), set()
+        me = len(ops)
+        for k in dict.fromkeys(list(reads) + list(writes)):
+            if k[0] == "P":
+                if k in bank:
+                    d = bank[k]
+                    (deps if ops[d]["eng"] != eng or alt or ops[d]["alt"] else soft).add(d)
+                bank[k] = me
+            else:
+                if k in last_w:
+                    deps.add(last_w[k])
+                if k in writes:
+                    deps.update(readers.get(k, ()))
+        for k in reads:
+            readers.setdefault(k, set()).add(me)
+        for k in writes:
+            last_w[k] = me
+            readers[k] = set()
+        deps.discard(me)
+        ops.append({"eng": eng, "cost": cost, "deps": deps, "soft": soft - deps, "fns": fns, "sem": sem, "val": val, "lat": lat,
+                    "alt": alt, "b": now[0]})
+
+    def cv(n, two=False, half=False):
+        return max(64, n * (2 if two else 1) * (0.5 if half else 1)) * CYC
+    def cg(n):
+        return 0.05 + n * GAMMA * CYC
+    def vec(n, reads, writes, fn, two=False, half=False, gat=False):
+        op("V", cg(n) if gat else cv(n, two, half), reads, writes, [fn])
+    def acv(n, reads, writes, fa, fv=None, gat=False, half=False):
+        op("A", 0.065 + n * GAMMA * CYC if gat else max(64, n) * CYC, reads, writes, [fa],
+           alt=None if fv is None else ("V", cg(n) if gat else cv(n, half=half), [fv]))
+    def ts(o, i, s1, s2, o0, o1=None):
+        if o1 is None:
+            return lambda e: e.tensor_scalar(o, i, s1, None, o0)
+        return lambda e: e.tensor_scalar(o, i, s1, s2, o0, o1)
+    def tt(o, a, c, f):
+        return lambda e: e.tensor_tensor(o, a, c, f)
+    def cp(o, i):
+        return lambda e: e.tensor_copy(o, i)
+    def fill(o, c):
+        return lambda e: e.memset(o, c)
+    def act(o, i, f=F.Identity, bias=0.0, scale=1.0):
+        return lambda e: e.activation(o, i, f, bias=bias, scale=scale)
+    def mm(o, l, r, st, sp):
+        return lambda e: e.matmul(o, l, r, st, sp)
+    def pe(cycles, reads, writes, fns):
+        op("P", cycles * PCYC + 0.02, reads, writes, fns)
+
+    nload = [0]
+    def dma(q, o, i, reads, writes, us):
+        s = LOADS[nload[0]]
+        nload[0] += 1
+        op(q, 0.06, reads, writes, [lambda e: e.dma_start(o, i).then_inc(T.sem[s], 16)], s, 16, us)
+
+    dma("S", T.v0i[:, :], T.v0[:, :], (), ("v0i",), 2.0)
+    dma("S", T.j0i[:, :], T.j0[:, :], (), ("j0i",), 2.0)
+    for c in range(WCH):
+        s = slice(c * V // WCH, (c + 1) * V // WCH)
+        dma("S", T.win[0:128:2, s], T.adj[:, s], (), ("win0%d" % c,), 3.5 + 2 * c)
+        dma("A", T.win[1:128:2, s], T.adj[:, s], (), ("win1%d" % c,), 3.5 + 2 * c)
+    dma("S", T.hs[:, :], T.h[:, :], (), ("hs",), 9.0)
+    dma("S", T.y0s[:, :], T.y0[:, :], (), ("y0s",), 9.0)
+    dma("S", T.c0s[:, :], T.c0[:, :], (), ("c0s",), 9.0)
+    dma("S", T.xw[:, :], T.x[:, :], (), ("xw",), 12.0)
+    for c in range(WCH):
+        s = slice(c * V // WCH, (c + 1) * V // WCH)
+        vec(V // WCH, ("win0%d" % c, "win1%d" % c), ("wf%d" % c,), ts(T.wf[:, s], T.win[:, s], HALF, None, I.subtract))
+    WF = tuple("wf%d" % c for c in range(WCH))
+
+    def iota(name, pattern, base, cm, n, buf=None, key=None):
+        o = T[name][:, :] if buf is None else buf
+        if SCRATCH[name][2] == "int32":
+            fn = lambda e: e.iota(o, pattern, base, cm)
+        else:
+            fn = lambda e: e.iota(o, pattern, base, cm, allow_small_or_imprecise_dtypes=True)
+        op("G", 0.13 + 2 * n * CYC, (), (key or name,), [fn])
+    iota("ip", [[0, 1]], 0, 1, 1)
+    iota("rg8", [[1, 8]], 0, 0, 8)
+    iota("pc", [[-32, 4], [-8, 2]], 0, 1, 8)
+    iota("iv0", [[2, 4], [1, 4], [16, 8]], 0, 0, 128)
+    iota("iv1", [[2, 4], [1, 4], [16, 8]], 8, 0, 128)
+    iota("r128", [[1, 8], [0, 16]], 0, 0, 128)
+    iota("mi", [[1, 128]], 0, 0, 128)
+    iota("kc", [[-1, 8], [0, 2 * KK]], 0, 0, 16 * KK)
+    for b in range(NB):
+        iota("cd", [[0, 16 * W]], 0, 0, 16 * W, T.cd[:, 16 * W * b:16 * W * (b + 1)], "cd%d" % b)
+    iota("re0", [[1, 8], [0, 8], [1000, 2]], 0, 0, 128)
+    iota("re1", [[1, 8], [0, 8], [1000, 2]], -1000, 0, 128)
+    iota("iw", [[1, IW]], -int(HALF), 0, IW)
+
+    ti, cf = T.ti, T.cf
+    def c1(col):
+        return cf[:, col:col + 1]
+    PF, GC, EC, RC, S1, S2, S3, CODE1, CODE2, WC, P0, S3C = range(12)
+    vec(1, ("ip",), ("ti0",), ts(ti[:, 0:1], T.ip[:, :], 4, None, I.arith_shift_right))
+    vec(1, ("ip",), ("ti1",), ts(ti[:, 1:2], T.ip[:, :], 1, None, I.bitwise_and))
+    vec(1, ("ip",), ("ti2",), ts(ti[:, 2:3], T.ip[:, :], 1, 7, I.arith_shift_right, I.bitwise_and))
+    vec(1, ("ip",), ("cf0",), cp(c1(PF), T.ip[:, :]))
+    vec(3, ("ti0", "ti1", "ti2"), ("cf1",), cp(cf[:, 1:4], ti[:, 0:3]))
+    vec(1, ("ti2",), ("ti3",), ts(ti[:, 3:4], ti[:, 2:3], -1, None, I.mult))
+    vec(1, ("ti3",), ("ti4",), ts(ti[:, 4:5], ti[:, 3:4], 7, None, I.bitwise_and))
+    vec(1, ("ti4",), ("cf8",), cp(c1(CODE2), ti[:, 4:5]))
+    vec(1, ("cf1",), ("cf4",), ts(c1(S1), c1(EC), -1.0, 1.0, I.mult, I.add))
+    vec(1, ("cf1",), ("cf5",), ts(c1(S2), c1(EC), -16384.0, 8192.0, I.mult, I.add))
+    vec(1, ("cf1",), ("cf6",), ts(c1(S3), c1(EC), 8192.0, -8192.0 + HALF, I.mult, I.add))
+    vec(1, ("cf1",), ("cf11",), ts(c1(S3C), c1(EC), 8192.0, -8192.0, I.mult, I.add))
+    vec(1, ("cf1",), ("cf7",), tt(c1(CODE1), c1(RC), c1(EC), I.subtract))
+    vec(1, ("cf1", "cf4"), ("cf9",), ts(c1(WC), c1(RC), 1.0, c1(S1), I.add, I.mult))
+    vec(1, ("cf0",), ("cf10",), ts(c1(P0), c1(PF), 0.0, None, I.is_equal))
+    for k in range(2):
+        vec(128, ("iv%d" % k, "cf0"), ("vi%d" % k,), ts(T["vi%d" % k][:, :], T["iv%d" % k][:, :], c1(PF), None, I.is_equal))
+    vec(8, ("rg8", "cf1"), ("mk",), ts(T.mk[:, :], T.rg8[:, :], c1(GC), None, I.is_equal))
+    vec(8, ("mk",), ("mk8",), ts(T.mk8[:, :], T.mk[:, :], 8.0, None, I.mult))
+    for name, sc, dep in (("ep0", c1(S1), "cf4"), ("ep1", c1(EC), "cf1"), ("ow", 8.0, "mk"), ("jp", c1(WC), "cf9"), ("hp", None, "hs")):
+        buf = T[name]
+        vec(24, ("mi",), (name,), ts(buf[:, :], T.mi[:, 0:24], 0.0, None, I.mult))
+        for o in (0, 16):
+            vec(8, ("mk", dep), (name,), ts(buf[:, o:o + 8], T.mk[:, :], T.hs[:, :] if sc is None else sc, None, I.mult))
+    for qr in range(8):
+        vec(128, ("r128", "pc"), ("bc",), ts(T.bc[:, 128 * qr:128 * qr + 128], T.r128[:, :], T.pc[:, qr:qr + 1], None, I.is_equal))
+    vec(128, (), ("zb",), fill(T.zb[:, :], 0.0), half=True)
+    vec(128, ("mi", "cf0"), ("idb",), ts(T.idb[:, :], T.mi[:, :], c1(PF), None, I.is_equal))
+    vec(128, ("r128", "cf1", "cf9"), ("jwc",), ts(T.jwc[:, :], T.r128[:, :], c1(GC), c1(WC), I.is_equal, I.mult))
+    for k in range(2):
+        pm = T["pm%d" % k]
+        vec(128, ("mi",), ("pm%d" % k,), ts(pm[:, :], T.mi[:, :], 0.0, None, I.mult))
+        for qr in range(8):
+            vec(8, ("rg8", "pc"), ("pm%d" % k,), ts(pm[:, 8 * k + qr:128:16], T.rg8[:, :], T.pc[:, qr:qr + 1], None, I.is_equal))
+    vec(128, ("mi", "cf10"), ("r0b",), ts(T.r0b[:, :], T.mi[:, :], 0.0, c1(P0), I.mult, I.add))
+    for qr in range(8):
+        for e_ in range(2):
+            o = 128 * (2 * qr + e_)
+            vec(128, ("re%d" % e_, "pc"), ("bce",), ts(T.bce[:, o:o + 128], T["re%d" % e_][:, :], T.pc[:, qr:qr + 1], None, I.is_equal))
+    vec(16, ("v0i",), ("v0f",), ts(T.v0f[:, :], T.v0i[:, :], HALF, None, I.subtract))
+    vec(16, ("j0i",), ("j0f",), cp(T.j0f[:, :], T.j0i[:, :]))
+
+    HJ, HE, HO, HP, HA = 0, KK, 3 * KK, 5 * KK, 7 * KK
+
+    def v(n, lo=0, hi=None, st=1):
+        w = SIZE[n]
+        b = now[0]
+        if n not in SCRATCH:
+            n, b = "%s_%d" % (n, b), 0
+        return T[n][:, b * w + lo:b * w + (w if hi is None else hi):st]
+
+    def c2h(out, oc, src, so, pads, into=False):
+        r = []
+        for q in range(4):
+            for rr in range(2):
+                r.append(mm(out[32 * q:32 * q + 16, oc:oc + KK], pads[:, 8 * rr:8 * rr + 16], v(src, so + 2 * q + rr, so + W, 8),
+                            not into and rr == 0, not into and rr == 1))
+        return r
+
+    def h2l(out, oc, srcs, n):
+        r = [(T["pm%d" % k], v(s, k, n * KK, 2)) for s in srcs for k in range(2)]
+        return [mm(out[:, oc:oc + n * ML], m[:, :], s, i == 0, i == len(r) - 1) for i, (m, s) in enumerate(r)]
+
+    def tools(b):
+        now[0] = b
+        return ([T["%s_%d" % (n, b)] for n in ("PS", "PC", "PH", "PL")], (lambda n: n + str(b)), [("P", n, b) for n in "SCHL"])
+
+    def again(b, y, ykey):
+        (S, C, H, L), K, (PS, PC, PH, PL) = tools(b)
+        pe(8 * 16, (ykey, "hp"), (PH,), c2h(H, HA, y, 0, T.hp))
+        vec(KK, (PH,), (K("ai"),), cp(v("ai"), H[:, HA:HA + KK]))
+        vec(KK, (K("ai"),), (K("aj"),), ts(v("aj"), v("ai"), V - 1, None, I.bitwise_and))
+        vec(KK, (K("aj"),), (K("ag"),), ts(v("ag"), v("aj"), HALF, None, I.subtract))
+
+    def blockdiag(b):
+        _, K, _ = tools(b)
+        for q in range(8):
+            o, i, s = v("cd", q, 16 * W, 16), v("cc", 0, W), T.mk8[:, q:q + 1]
+            acv(W, (K("cc0"), "mk8", K("cd")), (K("cd_%d_" % q),), act(o, i, F.Copy, 0.0, s), ts(o, i, s, None, I.mult), half=True)
+
+    def start(b):
+        (S, C, H, L), K, (PS, PC, PH, PL) = tools(b)
+        s = slice(b * ML, (b + 1) * ML)
+        vec(8 * KK, (), (PH,), fill(H[:, 0:8 * KK], 0.0))
+        vec(ML, ("v0i",), (K("lv"),), cp(v("lv"), T.v0i[:, s]))
+        for bk, key, src in ((H, PH, T.j0f), (C, PC, T.v0f)):
+            pe(128, ("v0f", "j0f", "vi0", "vi1"), (key,), [mm(bk[:, k:KK:2], T["vi%d" % k][:, :], src[:, s], True, True) for k in range(2)])
+        vec(KK, (PH,), (K("jb"),), cp(v("jb"), H[:, HJ:HJ + KK]))
+        for k in range(2):
+            vec(KK, (PC,), (K("vv"),), cp(v("vv", k * KK, (k + 1) * KK), C[:, 0:KK]))
+        vec(2 * KK, (), (K("te"),), fill(v("te"), 0.0))
+        for k in range(2):
+            vec(W, ("c0s",), (K("cc%d" % k),), cp(v("cc", k * W, (k + 1) * W), v("c0s")), half=True)
+        blockdiag(b)
+        again(b, "y0s", "y0s")
+
+    def rows(b, first):
+        (S, C, H, L), K, (PS, PC, PH, PL) = tools(b)
+        fns = [mm(C[:, 0:W], T.zb[:, :], T.bc[:, 0:W], True, False)]
+        for qr in range(8):
+            fns.append(mm(C[:, qr:W:8], T.bc[:, 128 * qr:128 * qr + 128], v("jb"), False, False))
+        if first:
+            fns.append(mm(C[:, 0:W], T.zb[:, :], T.bc[:, 0:W], False, True))
+        pe(W + 8 * 64, ("zb", "bc", K("jb")), (PC,), fns)
+        if not first:
+            acv(W, ("iw", K("lu")), (K("uc"),), act(v("uc"), T.iw[:, :].indirect(v("lu"))), gat=True)
+            vec(W, WF + (K("lv"), K("uc")), (K("eq"),), tt(v("eq"), T.wf[:, :].indirect(v("lv")), v("uc"), I.is_equal), gat=True)
+            pe(W, (K("eq"), "jwc"), (PC,), [mm(C[:, 0:W], T.jwc[:, :], v("eq"), False, True)])
+
+    def step(b, first):
+        (S, C, H, L), K, (PS, PC, PH, PL) = tools(b)
+        rows(b, first)
+        vr = T.wf[:, :].indirect(v("lv"))
+        acv(W, WF + (K("lv"),), (K("av"),), act(v("av"), vr), cp(v("av"), vr), gat=True)
+        vec(W, (PC, "cf7"), (PC, K("m1")), ts(C[:, 0:W], C[:, 0:W], c1(CODE1), None, I.is_equal))
+        vec(W, (PC, K("av"), K("m1")), (K("pr1"),), tt(v("pr1"), v("av"), C[:, 0:W], I.mult))
+        if not first:
+            pe(128 + 8 * 16, (K("eq"), "jp", "idb", "zb", K("jb")), (PH,),
+               [mm(H[:, HJ:HJ + KK], T.zb[:, :], v("jb"), True, False)] + c2h(H, HJ, "eq", 0, T.jp, True)
+               + [mm(H[:, HJ:HJ + KK], T.idb[:, :], v("jb"), False, True)])
+        vec(KK, (PH,), (K("bk"),), ts(v("bk"), H[:, HJ:HJ + KK], 8.0, None, I.is_ge))
+        vec(KK, (PH,), (K("ok0"),), ts(v("ok", 0, KK), H[:, HJ:HJ + KK], 8.0, None, I.is_lt))
+        vec(KK, (PH,), (K("ok1"),), ts(v("ok", KK, 2 * KK), H[:, HJ:HJ + KK], 7.0, None, I.is_lt))
+        acv(KK, (PH,), (K("j2"),), act(v("j2"), H[:, HJ:HJ + KK], F.Copy, 2.0))
+        vec(KK, (K("bk"), K("vv")), (K("te"),), tt(v("te", 0, KK), v("bk"), v("vv", 0, KK), I.mult))
+        pe(16 * 16, (K("pr1"), "ep0", "ep1"), (PH,), c2h(H, HE, "pr1", 0, T.ep0) + c2h(H, HE + KK, "pr1", 0, T.ep1))
+        vec(2 * KK, (PH, K("te")), (K("eh"),), tt(v("eh"), H[:, HE:HE + 2 * KK], v("te"), I.add))
+        pe(128, (K("eh"), "pm0", "pm1"), (PL,), h2l(L, 0, ["eh"], 2))
+        vec(2 * ML, (PL,), (K("le"),), ts(v("le"), L[:, 0:2 * ML], HALF, None, I.add))
+        w1, w2 = T.wf[:, :].indirect(v("le", 0, ML)), T.wf[:, :].indirect(v("le", ML, 2 * ML))
+        acv(W, WF + (K("le"), "cf4", "cf5"), (K("zz"),), act(v("zz"), w1, F.Identity, c1(S2), c1(S1)), ts(v("zz"), w1, c1(S1), c1(S2), I.mult, I.add), gat=True)
+        vec(W, WF + (K("le"), K("zz")), (K("bb"),), tt(v("bb"), w2, v("zz"), I.max), gat=True)
+        vec(W, (K("bb"), "cf6"), (K("lb"),), ts(v("lb"), v("bb"), c1(S3), None, I.add))
+        pe(16 * KK, ("r0b", "kc"), (PS,), [mm(S[:, 0:16 * KK], T.r0b[:, :], T.kc[:, :], True, False)])
+        for c in range(NCH):
+            o, i = v("xg", 16 * CH * c, 16 * CH * (c + 1)), T.xw[:, :].indirect(v("lb", CH * c, CH * (c + 1)))
+            acv(16 * CH, ("xw", K("lb")), (K("xg%d_" % c),), act(o, i), cp(o, i), gat=True)
+            if c == 0:
+                vec(2 * W, ("xw", K("le"), K("cc0"), K("cc1")), (K("po"),), tt(v("po"), T.xw[:, :].indirect(v("le")), v("cc"), I.mult), gat=True)
+                pe(16 * 16, (K("po"), "ow"), (PH,), c2h(H, HO, "po", 0, T.ow) + c2h(H, HO + KK, "po", W, T.ow))
+                acv(W, (K("bb"), "cf11"), (K("bq"),), act(v("bq"), v("bb"), F.Identity, c1(S3C)), ts(v("bq"), v("bb"), c1(S3C), None, I.add))
+                vec(2 * KK, (K("eh"), K("vv")), (K("dd"),), tt(v("dd"), v("eh"), v("vv"), I.subtract))
+                vec(KK, (K("j2"), K("ok0")), (K("jq"),), tt(v("jq"), v("j2"), v("ok", 0, KK), I.mult))
+                vec(KK, (K("vv"), K("ok0")), (K("vk"),), tt(v("vk"), v("vv", 0, KK), v("ok", 0, KK), I.mult))
+            fns = []
+            for la in range(CH * c, CH * (c + 1)):
+                q, rr, k = (la % 8) // 2, la % 2, la // 8
+                lo = 16 * la - 8 * rr
+                fns.append(mm(S[32 * q:32 * q + 16, k:16 * KK:KK], v("cd", lo, lo + 16), v("xg", 16 * la, 16 * la + 16), False, False))
+            if c == NCH - 1:
+                fns.append(mm(S[:, 0:16 * KK], T.zb[:, :], T.kc[:, :], False, True))
+            pe(16 * CH, (K("xg%d_" % c), K("cd"), "zb", "kc") + tuple(K("cd_%d_" % q) for q in range(8)), (PS,), fns)
+        hf = 8 * KK
+        acv(hf, (PS,), (K("ta"),), act(v("ta"), S[:, hf:2 * hf]), cp(v("ta"), S[:, hf:2 * hf]))
+        vec(hf, (PS, K("ta")), (K("tb"),), tt(v("tb"), S[:, 0:hf], v("ta"), I.max))
+        vec(hf // 2, (K("tb"),), (K("tc"),), tt(v("tc"), v("tb", 0, hf // 2), v("tb", hf // 2, hf), I.max), two=True)
+        vec(hf // 4, (K("tc"),), (K("t3"),), tt(v("t3"), v("tc", 0, hf // 4), v("tc", hf // 4, hf // 2), I.max), two=True)
+        vec(2 * KK, (K("t3"),), (K("ri"),), ts(v("ri"), v("t3"), 7, None, I.bitwise_and))
+        vec(2 * KK, (K("ri"),), (K("rb"),), cp(v("rb"), v("ri")))
+        fns = []
+        for qr in range(8):
+            for e_ in range(2):
+                o = 128 * (2 * qr + e_)
+                fns.append(mm(C[:, W + qr:2 * W:8], T.bce[:, o:o + 128], v("rb", e_ * KK, (e_ + 1) * KK), e_ == 0, e_ == 1))
+        pe(1024, (K("rb"), "bce"), (PC,), fns)
+        vec(2 * KK, (K("t3"), PH), (K("gt"),), tt(v("gt"), v("t3"), H[:, HO:HO + 2 * KK], I.is_gt))
+        vec(W, (PC, "cf8"), (PC, K("m2")), ts(C[:, W:2 * W], C[:, W:2 * W], c1(CODE2), None, I.is_equal))
+        vec(W, (PC, K("bq"), K("m2")), (K("pr2"),), tt(v("pr2"), v("bq"), C[:, W:2 * W], I.mult))
+        vec(KK, (K("gt"), K("bk")), (K("up"),), tt(v("up"), v("gt", 0, KK), v("bk"), I.mult))
+        vec(KK, (K("up"), K("vv")), (K("us"),), tt(v("us"), v("up"), v("vv", 0, KK), I.mult))
+        vec(KK, (K("up"),), (K("nu"),), ts(v("nu"), v("up"), 0.0, HALF, I.is_equal, I.mult))
+        pe(256, (K("us"), K("nu"), "pm0", "pm1"), (PL,), h2l(L, 2 * ML, ["us", "nu"], 1))
+        pe(16 * 16, (K("pr2"), "ep0", "ep1"), (PH,), c2h(H, HP, "pr2", 0, T.ep0) + c2h(H, HP + KK, "pr2", 0, T.ep1))
+        vec(2 * KK, (K("gt"), K("ok0"), K("ok1")), (K("gk"),), tt(v("gk"), v("gt"), v("ok"), I.mult))
+        vec(KK, (K("bk"), K("up")), (K("tp"),), tt(v("tp"), v("bk"), v("up"), I.subtract))
+        vec(KK, (K("tp"), K("ag")), (K("at"),), tt(v("at"), v("tp"), v("ag"), I.mult))
+        vec(KK, (K("at"), K("vk")), (K("ba"),), tt(v("ba"), v("at"), v("vk"), I.add))
+        vec(ML, (PL,), (K("lu"),), ts(v("lu"), L[:, 2 * ML:3 * ML], HALF, None, I.add))
+        vec(2 * KK, (PH, K("vv")), (K("hh"),), tt(v("hh"), H[:, HP:HP + 2 * KK], v("vv"), I.is_equal))
+        vec(KK, (PH, K("up")), (K("pu"),), tt(v("pu"), H[:, HP:HP + KK], v("up"), I.mult))
+        vec(2 * KK, (K("gk"), K("hh")), (K("hh"),), tt(v("hh"), v("hh"), v("gk"), I.mult))
+        vec(KK, (K("pu"), K("ba")), (K("ba"),), tt(v("ba"), v("ba"), v("pu"), I.add))
+        vec(KK, (K("hh"),), (K("hh"),), tt(v("hh", KK, 2 * KK), v("hh", KK, 2 * KK), v("hh", 0, KK), I.is_gt))
+        vec(2 * KK, (K("hh"), K("dd")), (K("hd"),), tt(v("hd"), v("hh"), v("dd"), I.mult))
+        vec(KK, (K("hd"), K("ba")), (K("sa"),), tt(v("sa"), v("hd", 0, KK), v("ba"), I.add))
+        vec(KK, (K("sa"), K("hd")), (K("vv"),), tt(v("vv", 0, KK), v("sa"), v("hd", KK, 2 * KK), I.add))
+        pe(128, (K("vv"), "pm0", "pm1"), (PL,), h2l(L, 3 * ML, ["vv"], 1))
+        vec(ML, (PL,), (K("lv"),), ts(v("lv"), L[:, 3 * ML:4 * ML], HALF, None, I.add))
+        vec(KK, (K("sa"), K("hd")), (K("vv"),), tt(v("vv", KK, 2 * KK), v("sa"), v("hd", KK, 2 * KK), I.add))
+        vec(KK, (K("hh"),), (K("ho"),), tt(v("ho"), v("hh", 0, KK), v("hh", KK, 2 * KK), I.is_equal))
+        vec(KK, (K("ho"), K("jq")), (K("jb"),), tt(v("jb"), v("ho"), v("jq"), I.mult))
+
+    def change(b, t):
+        _, K, _ = tools(b)
+        xn, yn = "xv%d" % t, "yv%d" % t
+        xk, yk = K(xn + "_"), K(yn + "_")
+        xv, yv, sem = v(xn), v(yn), "ar_%d_%d" % (b, t)
+        i = T.xw[:, :].indirect(v("lv"))
+        acv(W, ("xw", K("lv")), (xk,), act(xv, i), cp(xv, i), gat=True)
+        msk = sum(1 << e for e in engines_of(topo, core, nxt))
+        rid, pid = topo.addr(nxt)[:2]
+        op("G", 0.5, (xk,), (), [lambda e: e.remote_dma(yv, xv, T.sem[sem], T.sem.sent, pid, rid, msk)], "remote")
+        op("N", 0.0, (xk,), (yk,), [], sem, len(engines_of(topo, prv, core)), 3.5)
+        vec(W, (xk, yk), (K("dy"),), tt(v("dy"), yv, xv, I.subtract), two=True)
+        acv(W, (K("dy"),), (K("sg"),), act(v("sg"), v("dy"), F.Sign))
+        vec(W, (K("sg"), K("cc0")), (K("cn"),), tt(v("cn"), v("cc", 0, W), v("sg"), I.add), two=True)
+        if t == NCHG - 1:
+            vec(W, (K("cn"),), (K("co"),), ts(v("co_s"), v("cn"), 15.0, -15.0, I.min, I.max))
+            dma("S", T.co[:, b * W:(b + 1) * W], v("co_s"), (K("co"),), (K("out_c"),), 2.0)
+            return
+        for k in range(2):
+            vec(W, (K("cn"),), (K("cc%d" % k),), ts(v("cc", k * W, (k + 1) * W), v("cn"), 15.0, -15.0, I.min, I.max))
+        blockdiag(b)
+        again(b, yn, yk)
+
+    def finish(b):
+        (S, C, H, L), K, (PS, PC, PH, PL) = tools(b)
+        rows(b, False)
+        acv(W, ("iw", K("lv")), (K("vc"),), act(v("vo_s"), T.iw[:, :].indirect(v("lv")), F.Copy, HALF), gat=True)
+        w = slice(b * W, (b + 1) * W)
+        dma("S", T.vo[:, w], T.vo_s[0:128:16, w], (K("vc"),), (K("out_v"),), 2.0)
+        acv(W, (PC,), (K("jo"),), act(v("jo_s"), C[:, 0:W]), cp(v("jo_s"), C[:, 0:W]))
+        dma("S", T.jo[:, w], T.jo_s[0:128:16, w], (K("jo"),), (K("out_j"),), 2.0)
+
+    for b in range(NB):
+        start(b)
+    for s in range(1, STEPS + 1):
+        for b in range(NB):
+            step(b, s == 1)
+            if s % 2 == 0:
+                change(b, s // 2 - 1)
+    for b in range(NB):
+        finish(b)
+    return ops
+
+
+def schedule(ops, keep, near, lead, noise=None):
+    n = len(ops)
+    succ = [[] for _ in range(n)]
+    for i, o in enumerate(ops):
+        for d in o["deps"] | o["soft"]:
+            succ[d].append(i)
+    rest = [0.0] * n
+    for i in range(n - 1, -1, -1):
+        rest[i] = ops[i]["cost"] + ops[i]["lat"] + WAKE + max([rest[j] for j in succ[i]], default=0.0)
+    rest = [r + (lead if ops[i]["b"] == 0 else 0.0) + (noise[i] if noise else 0.0) for i, r in enumerate(rest)]
+    left = [len(o["deps"] | o["soft"]) for o in ops]
+    ready, both = {q: [] for q in "VAPGSN"}, []
+    free = {q: 0.0 for q in "VAPGSN"}
+    at, start, eng = [0.0] * n, [0.0] * n, [o["eng"] for o in ops]
+    end_all = 0.0
+    def push(i):
+        (both if ops[i]["alt"] else ready[eng[i]]).append(i)
+    for i in range(n):
+        if not left[i]:
+            push(i)
+    for _ in range(n):
+        best = None
+        for q in "NPVASG":
+            cand = ready[q] + (both if q in "VA" else [])
+            if not cand:
+                continue
+            def when(i):
+                return max(free[q], at[i]) + (keep if q == "V" and ops[i]["alt"] else 0.0)
+            t0 = min(when(i) for i in cand) + near
+            i = max((i for i in cand if when(i) <= t0), key=lambda i: (rest[i], -i))
+            t = when(i)
+            if best is None or t < best[0]:
+                best = (t, q, i)
+        t, q, i = best
+        t = max(free[q], at[i])
+        o = ops[i]
+        (both if o["alt"] else ready[q]).remove(i)
+        cost = o["cost"]
+        if o["alt"]:
+            eng[i] = q
+            if q == "V":
+                cost = o["alt"][1]
+        if q != "N":
+            free[q] = t + cost
+        start[i] = t
+        end = t + cost + o["lat"]
+        end_all = max(end_all, end)
+        for j in succ[i]:
+            at[j] = max(at[j], end + WAKE if i in ops[j]["deps"] else t + cost)
+            left[j] -= 1
+            if not left[j]:
+                push(j)
+    return end_all, sorted(range(n), key=lambda i: (start[i], i)), eng
+
+
+def emit(g, T, ops, order, eng):
+    que = {"V": g.vector, "A": g.scalar, "P": g.tensor, "G": g, "S": g.sync}
+    cnt = {q: 0 for q in "VAPG"}
+    know = {q: {} for q in "VAPGS"}
+    after, pos = {}, {i: k for k, i in enumerate(order)}
+    for i in order:
+        o, q = ops[i], eng[i]
+        assert all(pos[d] < pos[i] for d in o["deps"] | o["soft"])
+        if q == "N":
+            after[i] = (o["sem"], o["val"], {o["sem"]: o["val"]})
+            continue
+        kn, need, src = know[q], {}, {}
+        for d in o["deps"]:
+            s, n, m = after[d]
+            if s is not None and kn.get(s, 0) < n and need.get(s, 0) < n:
+                need[s], src[s] = n, m
+        for s in sorted(need):
+            if not any(s2 != s and src[s2].get(s, 0) >= need[s] for s2 in need):
+                que[q].wait_ge(T.sem[s], need[s])
+        for s in need:
+            for s2, v2 in src[s].items():
+                kn[s2] = max(kn.get(s2, 0), v2)
+            kn[s] = max(kn.get(s, 0), need[s])
+        fns = o["alt"][2] if o["alt"] and q == "V" else o["fns"]
+        m = dict(kn)
+        if o["sem"] == "remote":
+            fns[0](que[q])
+            after[i] = (None, 0, {})
+        elif o["sem"] is not None:
+            fns[0](que[q])
+            m[o["sem"]] = o["val"]
+            after[i] = (o["sem"], o["val"], m)
+        else:
+            s = "s" + q
+            for fn in fns:
+                fn(que[q]).then_inc(T.sem[s], 1)
+                cnt[q] += 1
+            m[s] = cnt[q]
+            after[i] = (s, cnt[q], m)
+    return cnt
+
+
+PLANS = {}
+
+
+def plan(ops):
+    if "plan" not in PLANS:
+        best = min(((schedule(ops, k, n, l), (k, n, l)) for k in (0.3, 1.0, 2.0) for n in (0.02, 0.15, 0.3)
+                    for l in (0.0, 2.0, 6.0, 20.0)), key=lambda p: p[0][0])
+        rng, top, noise = np.random.default_rng(7), best[0], np.zeros(len(ops))
+        for t in range(100):
+            new = noise * 0.9 + rng.normal(0.0, 0.6, len(ops)) * (rng.random(len(ops)) < 0.2)
+            p = schedule(ops, best[1][0], best[1][1], best[1][2], [float(x) for x in new])
+            if p[0] < top[0]:
+                top, noise = p, new
+        PLANS["plan"] = top
+    return PLANS["plan"]
+
+
+def rank_program(g, core, T, topo):
+    rank = T.rank_of(core)
+    if rank is None:
+        return
+    ops = build(T, topo, core)
+    _, order, eng = plan(ops)
+    cnt = emit(g, T, ops, order, eng)
+    nxt = T.cores[(rank + 1) % len(T.cores)]
+    g.wait_ge(T.sem.sent, len(engines_of(topo, core, nxt)) * NB * NCHG)
+    for q in "VAPG":
+        g.wait_ge(T.sem["s" + q], cnt[q])
+    for i in order:
+        o = ops[i]
+        if o["sem"] is not None and o["sem"] != "remote":
+            g.wait_ge(T.sem[o["sem"]], o["val"])

@@ -3,6 +3,7 @@ from concourse.mybir import AluOpType as I, ActivationFunctionType as F
 
 V, STEPS, LANES = 4096, 8, 256
 HALF = 2048.0
+FAR = -1000000.0
 NB = 2
 W = LANES // NB
 ML = W // 16
@@ -23,15 +24,15 @@ def _b(dtype, **cols):
         SIZE[n] = cols[n]
         SCRATCH[n] = ("sbuf", [128, NB * cols[n]], dtype)
 _d("sbuf", "int32", win=V, v0i=16, j0i=16, ip=1, ti=8)
-_d("sbuf", "float32", wf=V, iw=IW, cf=16, r128=128, re0=128, re1=128, iv0=128, iv1=128, mi=128, rg8=8, pc=8, mk=8, mk8=8)
-_d("sbuf", "bfloat16", xw=V, hs=1, ow=24, jp=24, hp=24, jwc=128, bc=1024, bce=2048, r0b=128, zb=128, idb=128, kc=16 * KK)
+_d("sbuf", "float32", wf=V, iw=IW, cf=16, r128=128, re0=128, re1=128, iv0=128, iv1=128, mi=128, r8=128, rs=128, sa1=128, sa2=128,
+   rg8=8, pc=8, mk=8)
+_d("sbuf", "bfloat16", xw=V, hs=1, ow=24, jp=24, hp=24, jwc=128, bc=1024, bce=2048, r0b=128, zb=128, idb=128, k0=256, kc=256, sh=128)
 _d("sbuf", "float16", v0f=16, j0f=16, ep0=24, ep1=24, pm0=128, pm1=128, vi0=128, vi1=128)
-_b("float32", uc=W, av=W, zz=W, bb=W, bq=W, ta=8 * KK, tb=8 * KK, tc=4 * KK, te=2 * KK, ok=2 * KK, dd=2 * KK, gt=2 * KK, gk=2 * KK,
-   hh=2 * KK, hd=2 * KK, bk=KK, j2=KK, jq=KK, vk=KK, ag=KK, up=KK, tp=KK, at=KK, ba=KK, pu=KK, sa=KK, ho=KK,
-   dy=W, sg=W, cn=W, co_s=W, vo_s=W, jo_s=W)
-_b("float16", pr1=W, pr2=W, eh=2 * KK, vv=2 * KK, us=KK, nu=KK)
-_b("bfloat16", c0s=W, y0s=W, eq=W, po=2 * W, xg=16 * W, cc=2 * W, cd=16 * W, rb=2 * KK, jb=KK)
-_b("int32", t3=2 * KK, ri=2 * KK, ai=KK, aj=KK)
+_b("float32", uc=W, av=W, zz=W, bb=W, bq=W, sc=16 * KK, te=2 * KK, ok=2 * KK, gt=2 * KK, gk=2 * KK, ng=2 * KK, vg=2 * KK,
+   hh=2 * KK, nn=2 * KK, bk=KK, j2=KK, jq=KK, vk=KK, vy=KK, ag=KK, up=KK, u2=KK, tp=KK, g2=KK, vt=KK, dy=W, cn=W, co_s=W, vo_s=W, jo_s=W)
+_b("float16", pr1=W, pr2=W, eh=2 * KK, vv=2 * KK, nu=KK, un=KK, at=KK, pu=KK, s1=KK, a1=KK, a2=KK, s2=KK, yy=KK)
+_b("bfloat16", c0s=W, y0s=W, eq=W, po=2 * W, xg=16 * W, cc=2 * W, mb=W, cd=16 * W, rb=2 * KK, jb=KK)
+_b("int32", ri=2 * KK, ai=KK, aj=KK)
 _b("uint16", lv=ML, lu=ML, le=2 * ML, lb=W)
 for _k in range(NB):
     for _n in ("PS", "PC", "PH", "PL"):
@@ -44,7 +45,7 @@ for _k in range(NB):
 LOADS = ["d_%d" % k for k in range(6 + 2 * WCH + 3 * NB)]
 SEMAPHORES = ["sV", "sA", "sP", "sG", "sent"] + LOADS + ["ar_%d_%d" % (b, t) for b in range(NB) for t in range(NCHG)]
 
-CYC, PCYC, GAMMA, WAKE = 0.00083, 0.00042, 1.5, 0.08
+CYC, PCYC, GAMMA, WAKE = 0.00083, 0.00042, 1.5, 0.3
 
 
 def engines_of(topo, src, dst):
@@ -95,6 +96,8 @@ def build(T, topo, core):
         return lambda e: e.tensor_scalar(o, i, s1, s2, o0, o1)
     def tt(o, a, c, f):
         return lambda e: e.tensor_tensor(o, a, c, f)
+    def scan(o, a, c):
+        return lambda e: e.tensor_tensor_scan(o, a, c, FAR, I.add, I.max)
     def cp(o, i):
         return lambda e: e.tensor_copy(o, i)
     def fill(o, c):
@@ -141,7 +144,8 @@ def build(T, topo, core):
     iota("iv1", [[2, 4], [1, 4], [16, 8]], 8, 0, 128)
     iota("r128", [[1, 8], [0, 16]], 0, 0, 128)
     iota("mi", [[1, 128]], 0, 0, 128)
-    iota("kc", [[-1, 8], [0, 2 * KK]], 0, 0, 16 * KK)
+    iota("r8", [[0, 16], [1, 8]], 0, 0, 128)
+    iota("k0", [[0, 16], [-1, 8], [0, 2]], 0, 0, 256)
     for b in range(NB):
         iota("cd", [[0, 16 * W]], 0, 0, 16 * W, T.cd[:, 16 * W * b:16 * W * (b + 1)], "cd%d" % b)
     iota("re0", [[1, 8], [0, 8], [1000, 2]], 0, 0, 128)
@@ -151,27 +155,26 @@ def build(T, topo, core):
     ti, cf = T.ti, T.cf
     def c1(col):
         return cf[:, col:col + 1]
-    PF, GC, EC, RC, S1, S2, S3, CODE1, CODE2, WC, P0, S3C = range(12)
+    PF, GC, EC, RC, S1, S2, S3, CODE1, CODE2, WC, S3C, P0, PF2, PF5 = range(14)
     vec(1, ("ip",), ("ti0",), ts(ti[:, 0:1], T.ip[:, :], 4, None, I.arith_shift_right))
     vec(1, ("ip",), ("ti1",), ts(ti[:, 1:2], T.ip[:, :], 1, None, I.bitwise_and))
     vec(1, ("ip",), ("ti2",), ts(ti[:, 2:3], T.ip[:, :], 1, 7, I.arith_shift_right, I.bitwise_and))
     vec(1, ("ip",), ("cf0",), cp(c1(PF), T.ip[:, :]))
     vec(3, ("ti0", "ti1", "ti2"), ("cf1",), cp(cf[:, 1:4], ti[:, 0:3]))
-    vec(1, ("ti2",), ("ti3",), ts(ti[:, 3:4], ti[:, 2:3], -1, None, I.mult))
-    vec(1, ("ti3",), ("ti4",), ts(ti[:, 4:5], ti[:, 3:4], 7, None, I.bitwise_and))
-    vec(1, ("ti4",), ("cf8",), cp(c1(CODE2), ti[:, 4:5]))
+    vec(1, ("cf1",), ("cf8",), ts(c1(CODE2), c1(RC), -0.125, 0.4375, I.mult, I.add))
+    vec(1, ("cf0",), ("cf11",), ts(c1(P0), c1(PF), 0.0, None, I.is_equal))
+    vec(1, ("cf0",), ("cf12",), ts(c1(PF2), c1(PF), 2.0, None, I.add))
+    vec(1, ("cf0",), ("cf13",), ts(c1(PF5), c1(PF), 5.0, None, I.add))
     vec(1, ("cf1",), ("cf4",), ts(c1(S1), c1(EC), -1.0, 1.0, I.mult, I.add))
     vec(1, ("cf1",), ("cf5",), ts(c1(S2), c1(EC), -16384.0, 8192.0, I.mult, I.add))
     vec(1, ("cf1",), ("cf6",), ts(c1(S3), c1(EC), 8192.0, -8192.0 + HALF, I.mult, I.add))
-    vec(1, ("cf1",), ("cf11",), ts(c1(S3C), c1(EC), 8192.0, -8192.0, I.mult, I.add))
+    vec(1, ("cf1",), ("cf10",), ts(c1(S3C), c1(EC), 8192.0, -8192.0, I.mult, I.add))
     vec(1, ("cf1",), ("cf7",), tt(c1(CODE1), c1(RC), c1(EC), I.subtract))
-    vec(1, ("cf1", "cf4"), ("cf9",), ts(c1(WC), c1(RC), 1.0, c1(S1), I.add, I.mult))
-    vec(1, ("cf0",), ("cf10",), ts(c1(P0), c1(PF), 0.0, None, I.is_equal))
+    vec(1, ("cf1", "cf4"), ("cf9",), ts(c1(WC), c1(RC), -31.0, c1(S1), I.add, I.mult))
     for k in range(2):
         vec(128, ("iv%d" % k, "cf0"), ("vi%d" % k,), ts(T["vi%d" % k][:, :], T["iv%d" % k][:, :], c1(PF), None, I.is_equal))
     vec(8, ("rg8", "cf1"), ("mk",), ts(T.mk[:, :], T.rg8[:, :], c1(GC), None, I.is_equal))
-    vec(8, ("mk",), ("mk8",), ts(T.mk8[:, :], T.mk[:, :], 8.0, None, I.mult))
-    for name, sc, dep in (("ep0", c1(S1), "cf4"), ("ep1", c1(EC), "cf1"), ("ow", 8.0, "mk"), ("jp", c1(WC), "cf9"), ("hp", None, "hs")):
+    for name, sc, dep in (("ep0", c1(S1), "cf4"), ("ep1", c1(EC), "cf1"), ("ow", 1.0, "mk"), ("jp", c1(WC), "cf9"), ("hp", None, "hs")):
         buf = T[name]
         vec(24, ("mi",), (name,), ts(buf[:, :], T.mi[:, 0:24], 0.0, None, I.mult))
         for o in (0, 16):
@@ -186,7 +189,14 @@ def build(T, topo, core):
         vec(128, ("mi",), ("pm%d" % k,), ts(pm[:, :], T.mi[:, :], 0.0, None, I.mult))
         for qr in range(8):
             vec(8, ("rg8", "pc"), ("pm%d" % k,), ts(pm[:, 8 * k + qr:128:16], T.rg8[:, :], T.pc[:, qr:qr + 1], None, I.is_equal))
-    vec(128, ("mi", "cf10"), ("r0b",), ts(T.r0b[:, :], T.mi[:, :], 0.0, c1(P0), I.mult, I.add))
+    vec(128, ("mi", "cf11"), ("r0b",), ts(T.r0b[:, :], T.mi[:, :], 0.0, c1(P0), I.mult, I.add))
+    vec(256, ("k0",), ("kc",), ts(T.kc[:, :], T.k0[:, :], 0.125, 0.4375, I.mult, I.add), half=True)
+    vec(128, ("r8",), ("rs",), ts(T.rs[:, :], T.r8[:, :], 0.0, FAR, I.is_equal, I.mult))
+    vec(128, ("mi", "cf12", "cf4"), ("sa1",), ts(T.sa1[:, :], T.mi[:, :], c1(PF2), c1(S1), I.is_equal, I.mult))
+    vec(128, ("mi", "cf13", "cf4"), ("sa2",), ts(T.sa2[:, :], T.mi[:, :], c1(PF5), c1(S1), I.is_equal, I.mult))
+    vec(128, ("sa1", "sa2"), ("sa1",), tt(T.sa1[:, :], T.sa1[:, :], T.sa2[:, :], I.add), two=True)
+    vec(128, ("r128", "cf1"), ("sa2",), ts(T.sa2[:, :], T.r128[:, :], c1(GC), None, I.is_equal))
+    vec(128, ("sa1", "sa2"), ("sh",), tt(T.sh[:, :], T.sa1[:, :], T.sa2[:, :], I.mult), two=True)
     for qr in range(8):
         for e_ in range(2):
             o = 128 * (2 * qr + e_)
@@ -194,7 +204,7 @@ def build(T, topo, core):
     vec(16, ("v0i",), ("v0f",), ts(T.v0f[:, :], T.v0i[:, :], HALF, None, I.subtract))
     vec(16, ("j0i",), ("j0f",), cp(T.j0f[:, :], T.j0i[:, :]))
 
-    HJ, HE, HO, HP, HA = 0, KK, 3 * KK, 5 * KK, 7 * KK
+    HE, HO, HP, HA, HJ = 0, 2 * KK, 4 * KK, 6 * KK, 16 * KK
 
     def v(n, lo=0, hi=None, st=1):
         w = SIZE[n]
@@ -203,11 +213,11 @@ def build(T, topo, core):
             n, b = "%s_%d" % (n, b), 0
         return T[n][:, b * w + lo:b * w + (w if hi is None else hi):st]
 
-    def c2h(out, oc, src, so, pads, into=False):
+    def c2h(out, oc, src, pads, into=False, n=1):
         r = []
         for q in range(4):
             for rr in range(2):
-                r.append(mm(out[32 * q:32 * q + 16, oc:oc + KK], pads[:, 8 * rr:8 * rr + 16], v(src, so + 2 * q + rr, so + W, 8),
+                r.append(mm(out[32 * q:32 * q + 16, oc:oc + n * KK], pads[:, 8 * rr:8 * rr + 16], v(src, 2 * q + rr, n * W, 8),
                             not into and rr == 0, not into and rr == 1))
         return r
 
@@ -219,9 +229,11 @@ def build(T, topo, core):
         now[0] = b
         return ([T["%s_%d" % (n, b)] for n in ("PS", "PC", "PH", "PL")], (lambda n: n + str(b)), [("P", n, b) for n in "SCHL"])
 
+    late = {}
+
     def again(b, y, ykey):
         (S, C, H, L), K, (PS, PC, PH, PL) = tools(b)
-        pe(8 * 16, (ykey, "hp"), (PH,), c2h(H, HA, y, 0, T.hp))
+        pe(8 * 16, (ykey, "hp"), (PH,), c2h(H, HA, y, T.hp))
         vec(KK, (PH,), (K("ai"),), cp(v("ai"), H[:, HA:HA + KK]))
         vec(KK, (K("ai"),), (K("aj"),), ts(v("aj"), v("ai"), V - 1, None, I.bitwise_and))
         vec(KK, (K("aj"),), (K("ag"),), ts(v("ag"), v("aj"), HALF, None, I.subtract))
@@ -229,120 +241,123 @@ def build(T, topo, core):
     def blockdiag(b):
         _, K, _ = tools(b)
         for q in range(8):
-            o, i, s = v("cd", q, 16 * W, 16), v("cc", 0, W), T.mk8[:, q:q + 1]
-            acv(W, (K("cc0"), "mk8", K("cd")), (K("cd_%d_" % q),), act(o, i, F.Copy, 0.0, s), ts(o, i, s, None, I.mult), half=True)
+            o, i, s = v("cd", q, 16 * W, 16), v("cc", 0, W), T.mk[:, q:q + 1]
+            acv(W, (K("cc0"), "mk", K("cd")), (K("cd_%d_" % q),), act(o, i, F.Copy, 0.0, s), ts(o, i, s, None, I.mult), half=True)
 
     def start(b):
         (S, C, H, L), K, (PS, PC, PH, PL) = tools(b)
         s = slice(b * ML, (b + 1) * ML)
-        vec(8 * KK, (), (PH,), fill(H[:, 0:8 * KK], 0.0))
+        vec(7 * KK, (), (PH,), fill(H[:, 0:7 * KK], 0.0))
         vec(ML, ("v0i",), (K("lv"),), cp(v("lv"), T.v0i[:, s]))
-        for bk, key, src in ((H, PH, T.j0f), (C, PC, T.v0f)):
-            pe(128, ("v0f", "j0f", "vi0", "vi1"), (key,), [mm(bk[:, k:KK:2], T["vi%d" % k][:, :], src[:, s], True, True) for k in range(2)])
-        vec(KK, (PH,), (K("jb"),), cp(v("jb"), H[:, HJ:HJ + KK]))
+        pe(128, ("j0f", "vi0", "vi1"), (PS,), [mm(S[:, HJ + k:HJ + KK:2], T["vi%d" % k][:, :], T.j0f[:, s], True, True) for k in range(2)])
+        pe(128, ("v0f", "vi0", "vi1"), (PC,), [mm(C[:, k:KK:2], T["vi%d" % k][:, :], T.v0f[:, s], True, True) for k in range(2)])
+        vec(KK, (PS,), (K("jb"),), cp(v("jb"), S[:, HJ:HJ + KK]))
         for k in range(2):
             vec(KK, (PC,), (K("vv"),), cp(v("vv", k * KK, (k + 1) * KK), C[:, 0:KK]))
         vec(2 * KK, (), (K("te"),), fill(v("te"), 0.0))
         for k in range(2):
             vec(W, ("c0s",), (K("cc%d" % k),), cp(v("cc", k * W, (k + 1) * W), v("c0s")), half=True)
         blockdiag(b)
-        again(b, "y0s", "y0s")
+        late[b] = ("y0s", "y0s")
 
-    def rows(b, first):
-        (S, C, H, L), K, (PS, PC, PH, PL) = tools(b)
-        fns = [mm(C[:, 0:W], T.zb[:, :], T.bc[:, 0:W], True, False)]
-        for qr in range(8):
-            fns.append(mm(C[:, qr:W:8], T.bc[:, 128 * qr:128 * qr + 128], v("jb"), False, False))
-        if first:
-            fns.append(mm(C[:, 0:W], T.zb[:, :], T.bc[:, 0:W], False, True))
-        pe(W + 8 * 64, ("zb", "bc", K("jb")), (PC,), fns)
-        if not first:
-            acv(W, ("iw", K("lu")), (K("uc"),), act(v("uc"), T.iw[:, :].indirect(v("lu"))), gat=True)
-            vec(W, WF + (K("lv"), K("uc")), (K("eq"),), tt(v("eq"), T.wf[:, :].indirect(v("lv")), v("uc"), I.is_equal), gat=True)
-            pe(W, (K("eq"), "jwc"), (PC,), [mm(C[:, 0:W], T.jwc[:, :], v("eq"), False, True)])
+    def came(b):
+        _, K, _ = tools(b)
+        acv(W, ("iw", K("lu")), (K("uc"),), act(v("uc"), T.iw[:, :].indirect(v("lu"))), gat=True)
+        vec(W, WF + (K("lv"), K("uc")), (K("eq"),), tt(v("eq"), T.wf[:, :].indirect(v("lv")), v("uc"), I.is_equal), gat=True)
 
     def step(b, first):
         (S, C, H, L), K, (PS, PC, PH, PL) = tools(b)
-        rows(b, first)
+        pe(8 * 64, ("bc", K("jb")), (PC,), [mm(C[:, 2 * W + qr:3 * W:8], T.bc[:, 128 * qr:128 * qr + 128], v("jb"), True, True) for qr in range(8)])
+        vec(W, (PC, "cf7"), (K("mb"),), ts(v("mb"), C[:, 2 * W:3 * W], c1(CODE1), None, I.is_equal))
+        pe(W, (K("mb"), "idb"), (PC,), [mm(C[:, 0:W], T.idb[:, :], v("mb"), True, first)])
         vr = T.wf[:, :].indirect(v("lv"))
-        acv(W, WF + (K("lv"),), (K("av"),), act(v("av"), vr), cp(v("av"), vr), gat=True)
-        vec(W, (PC, "cf7"), (PC, K("m1")), ts(C[:, 0:W], C[:, 0:W], c1(CODE1), None, I.is_equal))
-        vec(W, (PC, K("av"), K("m1")), (K("pr1"),), tt(v("pr1"), v("av"), C[:, 0:W], I.mult))
         if not first:
-            pe(128 + 8 * 16, (K("eq"), "jp", "idb", "zb", K("jb")), (PH,),
-               [mm(H[:, HJ:HJ + KK], T.zb[:, :], v("jb"), True, False)] + c2h(H, HJ, "eq", 0, T.jp, True)
-               + [mm(H[:, HJ:HJ + KK], T.idb[:, :], v("jb"), False, True)])
-        vec(KK, (PH,), (K("bk"),), ts(v("bk"), H[:, HJ:HJ + KK], 8.0, None, I.is_ge))
-        vec(KK, (PH,), (K("ok0"),), ts(v("ok", 0, KK), H[:, HJ:HJ + KK], 8.0, None, I.is_lt))
-        vec(KK, (PH,), (K("ok1"),), ts(v("ok", KK, 2 * KK), H[:, HJ:HJ + KK], 7.0, None, I.is_lt))
-        acv(KK, (PH,), (K("j2"),), act(v("j2"), H[:, HJ:HJ + KK], F.Copy, 2.0))
+            came(b)
+            pe(W, (K("eq"), "sh"), (PC,), [mm(C[:, 0:W], T.sh[:, :], v("eq"), False, True)])
+        acv(W, WF + (K("lv"),), (K("av"),), act(v("av"), vr), cp(v("av"), vr), gat=True)
+        vec(W, (PC, K("av")), (K("pr1"),), tt(v("pr1"), v("av"), C[:, 0:W], I.mult))
+        J = S[:, HJ:HJ + KK]
+        if not first:
+            pe(128 + 8 * 16, (K("eq"), "jp", "idb", "zb", K("jb")), (PS,),
+               [mm(J, T.zb[:, :], v("jb"), True, False)] + c2h(S, HJ, "eq", T.jp, True) + [mm(J, T.idb[:, :], v("jb"), False, True)])
+        vec(KK, (PS,), (K("bk"),), ts(v("bk"), J, 8.0, None, I.is_ge))
         vec(KK, (K("bk"), K("vv")), (K("te"),), tt(v("te", 0, KK), v("bk"), v("vv", 0, KK), I.mult))
-        pe(16 * 16, (K("pr1"), "ep0", "ep1"), (PH,), c2h(H, HE, "pr1", 0, T.ep0) + c2h(H, HE + KK, "pr1", 0, T.ep1))
+        pe(16 * 16, (K("pr1"), "ep0", "ep1"), (PH,), c2h(H, HE, "pr1", T.ep0) + c2h(H, HE + KK, "pr1", T.ep1))
         vec(2 * KK, (PH, K("te")), (K("eh"),), tt(v("eh"), H[:, HE:HE + 2 * KK], v("te"), I.add))
         pe(128, (K("eh"), "pm0", "pm1"), (PL,), h2l(L, 0, ["eh"], 2))
         vec(2 * ML, (PL,), (K("le"),), ts(v("le"), L[:, 0:2 * ML], HALF, None, I.add))
+        vec(KK, (PS,), (K("ok0"),), ts(v("ok", 0, KK), J, 8.0, None, I.is_lt))
+        vec(KK, (PS,), (K("ok1"),), ts(v("ok", KK, 2 * KK), J, 7.0, None, I.is_lt))
+        vec(KK, (PS,), (K("j2"),), ts(v("j2"), J, 2.0, None, I.add))
         w1, w2 = T.wf[:, :].indirect(v("le", 0, ML)), T.wf[:, :].indirect(v("le", ML, 2 * ML))
         acv(W, WF + (K("le"), "cf4", "cf5"), (K("zz"),), act(v("zz"), w1, F.Identity, c1(S2), c1(S1)), ts(v("zz"), w1, c1(S1), c1(S2), I.mult, I.add), gat=True)
         vec(W, WF + (K("le"), K("zz")), (K("bb"),), tt(v("bb"), w2, v("zz"), I.max), gat=True)
         vec(W, (K("bb"), "cf6"), (K("lb"),), ts(v("lb"), v("bb"), c1(S3), None, I.add))
-        pe(16 * KK, ("r0b", "kc"), (PS,), [mm(S[:, 0:16 * KK], T.r0b[:, :], T.kc[:, :], True, False)])
+        pe(256, ("r0b", "kc"), (PS,), [mm(S[:, 0:16 * KK], T.r0b[:, :], T.kc[:, 0:16 * KK], True, False)])
         for c in range(NCH):
             o, i = v("xg", 16 * CH * c, 16 * CH * (c + 1)), T.xw[:, :].indirect(v("lb", CH * c, CH * (c + 1)))
             acv(16 * CH, ("xw", K("lb")), (K("xg%d_" % c),), act(o, i), cp(o, i), gat=True)
             if c == 0:
                 vec(2 * W, ("xw", K("le"), K("cc0"), K("cc1")), (K("po"),), tt(v("po"), T.xw[:, :].indirect(v("le")), v("cc"), I.mult), gat=True)
-                pe(16 * 16, (K("po"), "ow"), (PH,), c2h(H, HO, "po", 0, T.ow) + c2h(H, HO + KK, "po", W, T.ow))
-                acv(W, (K("bb"), "cf11"), (K("bq"),), act(v("bq"), v("bb"), F.Identity, c1(S3C)), ts(v("bq"), v("bb"), c1(S3C), None, I.add))
-                vec(2 * KK, (K("eh"), K("vv")), (K("dd"),), tt(v("dd"), v("eh"), v("vv"), I.subtract))
+                pe(8 * 32, (K("po"), "ow"), (PH,), c2h(H, HO, "po", T.ow, n=2))
+                acv(W, (K("bb"), "cf10"), (K("bq"),), act(v("bq"), v("bb"), F.Identity, c1(S3C)), ts(v("bq"), v("bb"), c1(S3C), None, I.add))
                 vec(KK, (K("j2"), K("ok0")), (K("jq"),), tt(v("jq"), v("j2"), v("ok", 0, KK), I.mult))
                 vec(KK, (K("vv"), K("ok0")), (K("vk"),), tt(v("vk"), v("vv", 0, KK), v("ok", 0, KK), I.mult))
             fns = []
             for la in range(CH * c, CH * (c + 1)):
                 q, rr, k = (la % 8) // 2, la % 2, la // 8
                 lo = 16 * la - 8 * rr
-                fns.append(mm(S[32 * q:32 * q + 16, k:16 * KK:KK], v("cd", lo, lo + 16), v("xg", 16 * la, 16 * la + 16), False, False))
+                fns.append(mm(S[32 * q:32 * q + 16, 16 * k:16 * k + 16], v("cd", lo, lo + 16), v("xg", 16 * la, 16 * la + 16), False, False))
             if c == NCH - 1:
-                fns.append(mm(S[:, 0:16 * KK], T.zb[:, :], T.kc[:, :], False, True))
+                fns.append(mm(S[:, 15:16 * KK:16], T.zb[:, :], T.kc[:, 0:KK], False, True))
             pe(16 * CH, (K("xg%d_" % c), K("cd"), "zb", "kc") + tuple(K("cd_%d_" % q) for q in range(8)), (PS,), fns)
-        hf = 8 * KK
-        acv(hf, (PS,), (K("ta"),), act(v("ta"), S[:, hf:2 * hf]), cp(v("ta"), S[:, hf:2 * hf]))
-        vec(hf, (PS, K("ta")), (K("tb"),), tt(v("tb"), S[:, 0:hf], v("ta"), I.max))
-        vec(hf // 2, (K("tb"),), (K("tc"),), tt(v("tc"), v("tb", 0, hf // 2), v("tb", hf // 2, hf), I.max), two=True)
-        vec(hf // 4, (K("tc"),), (K("t3"),), tt(v("t3"), v("tc", 0, hf // 4), v("tc", hf // 4, hf // 2), I.max), two=True)
-        vec(2 * KK, (K("t3"),), (K("ri"),), ts(v("ri"), v("t3"), 7, None, I.bitwise_and))
-        vec(2 * KK, (K("ri"),), (K("rb"),), cp(v("rb"), v("ri")))
+        for e_ in range(2):
+            vec(8 * KK, (PS, "rs"), (K("sc%d_" % e_),), scan(v("sc", 8 * KK * e_, 8 * KK * (e_ + 1)), T.rs[:, 0:8 * KK], S[:, e_:16 * KK:2]))
+        top = v("sc", 7, 16 * KK, 8)
+        vec(2 * KK, (K("sc0_"), K("sc1_")), (K("ri"),), cp(v("ri"), top))
+        vec(2 * KK, (K("ri"), K("sc0_"), K("sc1_")), (K("rb"),), tt(v("rb"), top, v("ri"), I.subtract))
         fns = []
         for qr in range(8):
             for e_ in range(2):
                 o = 128 * (2 * qr + e_)
                 fns.append(mm(C[:, W + qr:2 * W:8], T.bce[:, o:o + 128], v("rb", e_ * KK, (e_ + 1) * KK), e_ == 0, e_ == 1))
         pe(1024, (K("rb"), "bce"), (PC,), fns)
-        vec(2 * KK, (K("t3"), PH), (K("gt"),), tt(v("gt"), v("t3"), H[:, HO:HO + 2 * KK], I.is_gt))
+        vec(2 * KK, (K("ri"), PH), (K("gt"),), tt(v("gt"), v("ri"), H[:, HO:HO + 2 * KK], I.is_gt))
+        if b in late:
+            again(b, *late.pop(b))
         vec(W, (PC, "cf8"), (PC, K("m2")), ts(C[:, W:2 * W], C[:, W:2 * W], c1(CODE2), None, I.is_equal))
         vec(W, (PC, K("bq"), K("m2")), (K("pr2"),), tt(v("pr2"), v("bq"), C[:, W:2 * W], I.mult))
         vec(KK, (K("gt"), K("bk")), (K("up"),), tt(v("up"), v("gt", 0, KK), v("bk"), I.mult))
-        vec(KK, (K("up"), K("vv")), (K("us"),), tt(v("us"), v("up"), v("vv", 0, KK), I.mult))
-        vec(KK, (K("up"),), (K("nu"),), ts(v("nu"), v("up"), 0.0, HALF, I.is_equal, I.mult))
-        pe(256, (K("us"), K("nu"), "pm0", "pm1"), (PL,), h2l(L, 2 * ML, ["us", "nu"], 1))
-        pe(16 * 16, (K("pr2"), "ep0", "ep1"), (PH,), c2h(H, HP, "pr2", 0, T.ep0) + c2h(H, HP + KK, "pr2", 0, T.ep1))
+        vec(KK, (K("up"),), (K("nu"),), ts(v("nu"), v("up"), -2 * HALF, HALF, I.mult, I.add))
+        vec(KK, (K("nu"), K("vv")), (K("un"),), tt(v("un"), v("nu"), v("vv", 0, KK), I.max))
+        pe(128, (K("un"), "pm0", "pm1"), (PL,), h2l(L, 2 * ML, ["un"], 1))
+        pe(16 * 16, (K("pr2"), "ep0", "ep1"), (PH,), c2h(H, HP, "pr2", T.ep0) + c2h(H, HP + KK, "pr2", T.ep1))
         vec(2 * KK, (K("gt"), K("ok0"), K("ok1")), (K("gk"),), tt(v("gk"), v("gt"), v("ok"), I.mult))
+        acv(KK, (K("up"),), (K("u2"),), act(v("u2"), v("up"), F.Copy, 0.0, 32.0))
+        vec(KK, (K("jq"), K("u2")), (K("jq"),), tt(v("jq"), v("jq"), v("u2"), I.add))
+        vec(2 * KK, (K("gk"),), (K("ng"),), ts(v("ng"), v("gk"), -8192.0, 8192.0, I.mult, I.add))
+        vec(2 * KK, (K("ng"), K("vv")), (K("vg"),), tt(v("vg"), v("ng"), v("vv"), I.add))
         vec(KK, (K("bk"), K("up")), (K("tp"),), tt(v("tp"), v("bk"), v("up"), I.subtract))
         vec(KK, (K("tp"), K("ag")), (K("at"),), tt(v("at"), v("tp"), v("ag"), I.mult))
-        vec(KK, (K("at"), K("vk")), (K("ba"),), tt(v("ba"), v("at"), v("vk"), I.add))
         vec(ML, (PL,), (K("lu"),), ts(v("lu"), L[:, 2 * ML:3 * ML], HALF, None, I.add))
-        vec(2 * KK, (PH, K("vv")), (K("hh"),), tt(v("hh"), H[:, HP:HP + 2 * KK], v("vv"), I.is_equal))
+        P2 = H[:, HP:HP + 2 * KK]
+        vec(2 * KK, (PH, K("vg")), (K("nn"),), tt(v("nn"), P2, v("vg"), I.not_equal))
+        vec(2 * KK, (PH, K("vg")), (K("hh"),), tt(v("hh"), P2, v("vg"), I.is_equal))
         vec(KK, (PH, K("up")), (K("pu"),), tt(v("pu"), H[:, HP:HP + KK], v("up"), I.mult))
-        vec(2 * KK, (K("gk"), K("hh")), (K("hh"),), tt(v("hh"), v("hh"), v("gk"), I.mult))
-        vec(KK, (K("pu"), K("ba")), (K("ba"),), tt(v("ba"), v("ba"), v("pu"), I.add))
-        vec(KK, (K("hh"),), (K("hh"),), tt(v("hh", KK, 2 * KK), v("hh", KK, 2 * KK), v("hh", 0, KK), I.is_gt))
-        vec(2 * KK, (K("hh"), K("dd")), (K("hd"),), tt(v("hd"), v("hh"), v("dd"), I.mult))
-        vec(KK, (K("hd"), K("ba")), (K("sa"),), tt(v("sa"), v("hd", 0, KK), v("ba"), I.add))
-        vec(KK, (K("sa"), K("hd")), (K("vv"),), tt(v("vv", 0, KK), v("sa"), v("hd", KK, 2 * KK), I.add))
-        pe(128, (K("vv"), "pm0", "pm1"), (PL,), h2l(L, 3 * ML, ["vv"], 1))
+        vec(KK, (K("hh"), K("nn")), (K("g2"),), tt(v("g2"), v("hh", KK, 2 * KK), v("nn", 0, KK), I.mult))
+        vec(KK, (K("vk"), K("nn")), (K("vy"),), tt(v("vy"), v("vk"), v("nn", 0, KK), I.mult))
+        vec(KK, (K("hh"), K("eh")), (K("a1"),), tt(v("a1"), v("hh", 0, KK), v("eh", 0, KK), I.mult))
+        vec(KK, (K("at"), K("pu")), (K("s1"),), tt(v("s1"), v("at"), v("pu"), I.add))
+        vec(KK, (K("jq"), K("nn")), (K("jq"),), tt(v("jq"), v("jq"), v("nn", 0, KK), I.mult))
+        vec(KK, (K("g2"), K("eh")), (K("a2"),), tt(v("a2"), v("g2"), v("eh", KK, 2 * KK), I.mult))
+        vec(KK, (K("vy"), K("nn")), (K("yy"),), tt(v("yy"), v("vy"), v("nn", KK, 2 * KK), I.mult))
+        vec(KK, (K("s1"), K("a1")), (K("s2"),), tt(v("s2"), v("s1"), v("a1"), I.add))
+        pe(64 * 6, (K("s2"), K("a2"), K("yy"), "pm0", "pm1"), (PL,), h2l(L, 3 * ML, ["s2", "a2", "yy"], 1))
         vec(ML, (PL,), (K("lv"),), ts(v("lv"), L[:, 3 * ML:4 * ML], HALF, None, I.add))
-        vec(KK, (K("sa"), K("hd")), (K("vv"),), tt(v("vv", KK, 2 * KK), v("sa"), v("hd", KK, 2 * KK), I.add))
-        vec(KK, (K("hh"),), (K("ho"),), tt(v("ho"), v("hh", 0, KK), v("hh", KK, 2 * KK), I.is_equal))
-        vec(KK, (K("ho"), K("jq")), (K("jb"),), tt(v("jb"), v("ho"), v("jq"), I.mult))
+        vec(KK, (K("jq"), K("nn")), (K("jb"),), tt(v("jb"), v("jq"), v("nn", KK, 2 * KK), I.mult))
+        vec(KK, (K("a2"), K("yy")), (K("vt"),), tt(v("vt"), v("a2"), v("yy"), I.add))
+        for k in range(2):
+            vec(KK, (K("vt"), K("s2")), (K("vv"),), tt(v("vv", k * KK, (k + 1) * KK), v("vt"), v("s2"), I.add))
 
     def change(b, t):
         _, K, _ = tools(b)
@@ -356,8 +371,8 @@ def build(T, topo, core):
         op("G", 0.5, (xk,), (), [lambda e: e.remote_dma(yv, xv, T.sem[sem], T.sem.sent, pid, rid, msk)], "remote")
         op("N", 0.0, (xk,), (yk,), [], sem, len(engines_of(topo, prv, core)), 3.5)
         vec(W, (xk, yk), (K("dy"),), tt(v("dy"), yv, xv, I.subtract), two=True)
-        acv(W, (K("dy"),), (K("sg"),), act(v("sg"), v("dy"), F.Sign))
-        vec(W, (K("sg"), K("cc0")), (K("cn"),), tt(v("cn"), v("cc", 0, W), v("sg"), I.add), two=True)
+        acv(W, (K("dy"),), (K("dy"),), act(v("dy"), v("dy"), F.Sign))
+        vec(W, (K("dy"), K("cc0")), (K("cn"),), tt(v("cn"), v("cc", 0, W), v("dy"), I.add), two=True)
         if t == NCHG - 1:
             vec(W, (K("cn"),), (K("co"),), ts(v("co_s"), v("cn"), 15.0, -15.0, I.min, I.max))
             dma("S", T.co[:, b * W:(b + 1) * W], v("co_s"), (K("co"),), (K("out_c"),), 2.0)
@@ -365,11 +380,15 @@ def build(T, topo, core):
         for k in range(2):
             vec(W, (K("cn"),), (K("cc%d" % k),), ts(v("cc", k * W, (k + 1) * W), v("cn"), 15.0, -15.0, I.min, I.max))
         blockdiag(b)
-        again(b, yn, yk)
+        late[b] = (yn, yk)
 
     def finish(b):
         (S, C, H, L), K, (PS, PC, PH, PL) = tools(b)
-        rows(b, False)
+        came(b)
+        fns = [mm(C[:, 0:W], T.zb[:, :], T.bc[:, 0:W], True, False)]
+        fns += [mm(C[:, qr:W:8], T.bc[:, 128 * qr:128 * qr + 128], v("jb"), False, False) for qr in range(8)]
+        pe(W + 8 * 64, ("zb", "bc", K("jb")), (PC,), fns)
+        pe(W, (K("eq"), "jwc"), (PC,), [mm(C[:, 0:W], T.jwc[:, :], v("eq"), False, True)])
         acv(W, ("iw", K("lv")), (K("vc"),), act(v("vo_s"), T.iw[:, :].indirect(v("lv")), F.Copy, HALF), gat=True)
         w = slice(b * W, (b + 1) * W)
         dma("S", T.vo[:, w], T.vo_s[0:128:16, w], (K("vc"),), (K("out_v"),), 2.0)
@@ -493,7 +512,7 @@ def plan(ops):
         best = min(((schedule(ops, k, n, l), (k, n, l)) for k in (0.3, 1.0, 2.0) for n in (0.02, 0.15, 0.3)
                     for l in (0.0, 2.0, 6.0, 20.0)), key=lambda p: p[0][0])
         rng, top, noise = np.random.default_rng(7), best[0], np.zeros(len(ops))
-        for t in range(100):
+        for t in range(300):
             new = noise * 0.9 + rng.normal(0.0, 0.6, len(ops)) * (rng.random(len(ops)) < 0.2)
             p = schedule(ops, best[1][0], best[1][1], best[1][2], [float(x) for x in new])
             if p[0] < top[0]:

import numpy as np
from concourse.mybir import AluOpType as I, ActivationFunctionType as F

V, STEPS, LANES = 4096, 8, 256
HALF = 2048.0
FAR = -1000000.0
NB = 2
W = LANES // NB
ML = W // 16
KK = W // 8
CH = 32
NCH = W // CH
IW = V + 8
NCHG = STEPS // 2
WCH = 4

SCRATCH = {}
SIZE = {}
def _d(where, dtype, **cols):
    for n in cols:
        SCRATCH[n] = (where, [128, cols[n]], dtype)
def _b(dtype, **cols):
    for n in cols:
        SIZE[n] = cols[n]
        SCRATCH[n] = ("sbuf", [128, NB * cols[n]], dtype)
_d("sbuf", "int32", win=V, v0i=16, j0i=16, ip=1, ti=8)
_d("sbuf", "float32", wf=V, iw=IW, cf=16, r128=128, re0=128, re1=128, iv0=128, iv1=128, mi=128, r8=128, rs=128, sa1=128, sa2=128,
   rg8=8, pc=8, mk=8)
_d("sbuf", "bfloat16", xw=V, hs=1, ow=24, jp=24, hp=24, jwc=128, bc=1024, bce=2048, r0b=128, zb=128, idb=128, k0=256, kc=256, sh=128)
_d("sbuf", "float16", v0f=16, j0f=16, ep0=24, ep1=24, pm0=128, pm1=128, vi0=128, vi1=128)
_b("float32", uc=W, av=W, zz=W, bb=W, bq=W, sc=16 * KK, te=2 * KK, ok=2 * KK, gt=2 * KK, gk=2 * KK, ng=2 * KK, vg=2 * KK,
   hh=2 * KK, nn=2 * KK, bk=KK, j2=KK, jq=KK, vk=KK, vy=KK, ag=KK, up=KK, u2=KK, tp=KK, g2=KK, vt=KK, dy=W, cn=W, co_s=W, vo_s=W, jo_s=W)
_b("float16", pr1=W, pr2=W, eh=2 * KK, vv=2 * KK, nu=KK, un=KK, at=KK, pu=KK, s1=KK, a1=KK, a2=KK, s2=KK, yy=KK)
_b("bfloat16", c0s=W, y0s=W, eq=W, po=2 * W, xg=16 * W, cc=2 * W, mb=W, cd=16 * W, rb=2 * KK, jb=KK)
_b("int32", ri=2 * KK, ai=KK, aj=KK)
_b("uint16", lv=ML, lu=ML, le=2 * ML, lb=W)
for _k in range(NB):
    for _n in ("PS", "PC", "PH", "PL"):
        SCRATCH["%s_%d" % (_n, _k)] = ("psum", [128, 512], "float32")
    for _t in range(NCHG):
        for _n in ("xv%d", "yv%d"):
            SIZE[_n % _t] = W
            SCRATCH[_n % _t + "_%d" % _k] = ("sbuf", [128, W], "bfloat16")

LOADS = ["d_%d" % k for k in range(6 + 2 * WCH + 3 * NB)]
SEMAPHORES = ["sV", "sA", "sP", "sG", "sent"] + LOADS + ["ar_%d_%d" % (b, t) for b in range(NB) for t in range(NCHG)]

CYC, PCYC, GAMMA, WAKE = 0.00083, 0.00042, 1.5, 0.3


def engines_of(topo, src, dst):
    return topo.engines(src, dst)[:8]


def build(T, topo, core):
    rank, n_ranks = T.rank_of(core), len(T.cores)
    nxt, prv = T.cores[(rank + 1) % n_ranks], T.cores[(rank - 1) % n_ranks]
    ops, last_w, readers, bank = [], {}, {}, {}
    now = [0]

    def op(eng, cost, reads, writes, fns, sem=None, val=0, lat=0.0, alt=None):
        deps, soft = set(), set()
        me = len(ops)
        for k in dict.fromkeys(list(reads) + list(writes)):
            if k[0] == "P":
                if k in bank:
                    d = bank[k]
                    (deps if ops[d]["eng"] != eng or alt or ops[d]["alt"] else soft).add(d)
                bank[k] = me
            else:
                if k in last_w:
                    deps.add(last_w[k])
                if k in writes:
                    deps.update(readers.get(k, ()))
        for k in reads:
            readers.setdefault(k, set()).add(me)
        for k in writes:
            last_w[k] = me
            readers[k] = set()
        deps.discard(me)
        ops.append({"eng": eng, "cost": cost, "deps": deps, "soft": soft - deps, "fns": fns, "sem": sem, "val": val, "lat": lat,
                    "alt": alt, "b": now[0]})

    def cv(n, two=False, half=False):
        return max(64, n * (2 if two else 1) * (0.5 if half else 1)) * CYC
    def cg(n):
        return 0.05 + n * GAMMA * CYC
    def vec(n, reads, writes, fn, two=False, half=False, gat=False):
        op("V", cg(n) if gat else cv(n, two, half), reads, writes, [fn])
    def acv(n, reads, writes, fa, fv=None, gat=False, half=False):
        op("A", 0.065 + n * GAMMA * CYC if gat else max(64, n) * CYC, reads, writes, [fa],
           alt=None if fv is None else ("V", cg(n) if gat else cv(n, half=half), [fv]))
    def ts(o, i, s1, s2, o0, o1=None):
        if o1 is None:
            return lambda e: e.tensor_scalar(o, i, s1, None, o0)
        return lambda e: e.tensor_scalar(o, i, s1, s2, o0, o1)
    def tt(o, a, c, f):
        return lambda e: e.tensor_tensor(o, a, c, f)
    def scan(o, a, c):
        return lambda e: e.tensor_tensor_scan(o, a, c, FAR, I.add, I.max)
    def cp(o, i):
        return lambda e: e.tensor_copy(o, i)
    def fill(o, c):
        return lambda e: e.memset(o, c)
    def act(o, i, f=F.Identity, bias=0.0, scale=1.0):
        return lambda e: e.activation(o, i, f, bias=bias, scale=scale)
    def mm(o, l, r, st, sp):
        return lambda e: e.matmul(o, l, r, st, sp)
    def pe(cycles, reads, writes, fns):
        op("P", cycles * PCYC + 0.02, reads, writes, fns)

    nload = [0]
    def dma(q, o, i, reads, writes, us):
        s = LOADS[nload[0]]
        nload[0] += 1
        op(q, 0.06, reads, writes, [lambda e: e.dma_start(o, i).then_inc(T.sem[s], 16)], s, 16, us)

    dma("S", T.v0i[:, :], T.v0[:, :], (), ("v0i",), 2.0)
    dma("S", T.j0i[:, :], T.j0[:, :], (), ("j0i",), 2.0)
    for c in range(WCH):
        s = slice(c * V // WCH, (c + 1) * V // WCH)
        dma("S", T.win[0:128:2, s], T.adj[:, s], (), ("win0%d" % c,), 3.5 + 2 * c)
        dma("A", T.win[1:128:2, s], T.adj[:, s], (), ("win1%d" % c,), 3.5 + 2 * c)
    dma("S", T.hs[:, :], T.h[:, :], (), ("hs",), 9.0)
    dma("S", T.y0s[:, :], T.y0[:, :], (), ("y0s",), 9.0)
    dma("S", T.c0s[:, :], T.c0[:, :], (), ("c0s",), 9.0)
    dma("S", T.xw[:, :], T.x[:, :], (), ("xw",), 12.0)
    for c in range(WCH):
        s = slice(c * V // WCH, (c + 1) * V // WCH)
        vec(V // WCH, ("win0%d" % c, "win1%d" % c), ("wf%d" % c,), ts(T.wf[:, s], T.win[:, s], HALF, None, I.subtract))
    WF = tuple("wf%d" % c for c in range(WCH))

    def iota(name, pattern, base, cm, n, buf=None, key=None):
        o = T[name][:, :] if buf is None else buf
        if SCRATCH[name][2] == "int32":
            fn = lambda e: e.iota(o, pattern, base, cm)
        else:
            fn = lambda e: e.iota(o, pattern, base, cm, allow_small_or_imprecise_dtypes=True)
        op("G", 0.13 + 2 * n * CYC, (), (key or name,), [fn])
    iota("ip", [[0, 1]], 0, 1, 1)
    iota("rg8", [[1, 8]], 0, 0, 8)
    iota("pc", [[-32, 4], [-8, 2]], 0, 1, 8)
    iota("iv0", [[2, 4], [1, 4], [16, 8]], 0, 0, 128)
    iota("iv1", [[2, 4], [1, 4], [16, 8]], 8, 0, 128)
    iota("r128", [[1, 8], [0, 16]], 0, 0, 128)
    iota("mi", [[1, 128]], 0, 0, 128)
    iota("r8", [[0, 16], [1, 8]], 0, 0, 128)
    iota("k0", [[0, 16], [-1, 8], [0, 2]], 0, 0, 256)
    for b in range(NB):
        iota("cd", [[0, 16 * W]], 0, 0, 16 * W, T.cd[:, 16 * W * b:16 * W * (b + 1)], "cd%d" % b)
    iota("re0", [[1, 8], [0, 8], [1000, 2]], 0, 0, 128)
    iota("re1", [[1, 8], [0, 8], [1000, 2]], -1000, 0, 128)
    iota("iw", [[1, IW]], -int(HALF), 0, IW)

    ti, cf = T.ti, T.cf
    def c1(col):
        return cf[:, col:col + 1]
    PF, GC, EC, RC, S1, S2, S3, CODE1, CODE2, WC, S3C, P0, PF2, PF5 = range(14)
    vec(1, ("ip",), ("ti0",), ts(ti[:, 0:1], T.ip[:, :], 4, None, I.arith_shift_right))
    vec(1, ("ip",), ("ti1",), ts(ti[:, 1:2], T.ip[:, :], 1, None, I.bitwise_and))
    vec(1, ("ip",), ("ti2",), ts(ti[:, 2:3], T.ip[:, :], 1, 7, I.arith_shift_right, I.bitwise_and))
    vec(1, ("ip",), ("cf0",), cp(c1(PF), T.ip[:, :]))
    vec(3, ("ti0", "ti1", "ti2"), ("cf1",), cp(cf[:, 1:4], ti[:, 0:3]))
    vec(1, ("cf1",), ("cf8",), ts(c1(CODE2), c1(RC), -0.125, 0.4375, I.mult, I.add))
    vec(1, ("cf0",), ("cf11",), ts(c1(P0), c1(PF), 0.0, None, I.is_equal))
    vec(1, ("cf0",), ("cf12",), ts(c1(PF2), c1(PF), 2.0, None, I.add))
    vec(1, ("cf0",), ("cf13",), ts(c1(PF5), c1(PF), 5.0, None, I.add))
    vec(1, ("cf1",), ("cf4",), ts(c1(S1), c1(EC), -1.0, 1.0, I.mult, I.add))
    vec(1, ("cf1",), ("cf5",), ts(c1(S2), c1(EC), -16384.0, 8192.0, I.mult, I.add))
    vec(1, ("cf1",), ("cf6",), ts(c1(S3), c1(EC), 8192.0, -8192.0 + HALF, I.mult, I.add))
    vec(1, ("cf1",), ("cf10",), ts(c1(S3C), c1(EC), 8192.0, -8192.0, I.mult, I.add))
    vec(1, ("cf1",), ("cf7",), tt(c1(CODE1), c1(RC), c1(EC), I.subtract))
    vec(1, ("cf1", "cf4"), ("cf9",), ts(c1(WC), c1(RC), -31.0, c1(S1), I.add, I.mult))
    for k in range(2):
        vec(128, ("iv%d" % k, "cf0"), ("vi%d" % k,), ts(T["vi%d" % k][:, :], T["iv%d" % k][:, :], c1(PF), None, I.is_equal))
    vec(8, ("rg8", "cf1"), ("mk",), ts(T.mk[:, :], T.rg8[:, :], c1(GC), None, I.is_equal))
    for name, sc, dep in (("ep0", c1(S1), "cf4"), ("ep1", c1(EC), "cf1"), ("ow", 1.0, "mk"), ("jp", c1(WC), "cf9"), ("hp", None, "hs")):
        buf = T[name]
        vec(24, ("mi",), (name,), ts(buf[:, :], T.mi[:, 0:24], 0.0, None, I.mult))
        for o in (0, 16):
            vec(8, ("mk", dep), (name,), ts(buf[:, o:o + 8], T.mk[:, :], T.hs[:, :] if sc is None else sc, None, I.mult))
    for qr in range(8):
        vec(128, ("r128", "pc"), ("bc",), ts(T.bc[:, 128 * qr:128 * qr + 128], T.r128[:, :], T.pc[:, qr:qr + 1], None, I.is_equal))
    vec(128, (), ("zb",), fill(T.zb[:, :], 0.0), half=True)
    vec(128, ("mi", "cf0"), ("idb",), ts(T.idb[:, :], T.mi[:, :], c1(PF), None, I.is_equal))
    vec(128, ("r128", "cf1", "cf9"), ("jwc",), ts(T.jwc[:, :], T.r128[:, :], c1(GC), c1(WC), I.is_equal, I.mult))
    for k in range(2):
        pm = T["pm%d" % k]
        vec(128, ("mi",), ("pm%d" % k,), ts(pm[:, :], T.mi[:, :], 0.0, None, I.mult))
        for qr in range(8):
            vec(8, ("rg8", "pc"), ("pm%d" % k,), ts(pm[:, 8 * k + qr:128:16], T.rg8[:, :], T.pc[:, qr:qr + 1], None, I.is_equal))
    vec(128, ("mi", "cf11"), ("r0b",), ts(T.r0b[:, :], T.mi[:, :], 0.0, c1(P0), I.mult, I.add))
    vec(256, ("k0",), ("kc",), ts(T.kc[:, :], T.k0[:, :], 0.125, 0.4375, I.mult, I.add), half=True)
    vec(128, ("r8",), ("rs",), ts(T.rs[:, :], T.r8[:, :], 0.0, FAR, I.is_equal, I.mult))
    vec(128, ("mi", "cf12", "cf4"), ("sa1",), ts(T.sa1[:, :], T.mi[:, :], c1(PF2), c1(S1), I.is_equal, I.mult))
    vec(128, ("mi", "cf13", "cf4"), ("sa2",), ts(T.sa2[:, :], T.mi[:, :], c1(PF5), c1(S1), I.is_equal, I.mult))
    vec(128, ("sa1", "sa2"), ("sa1",), tt(T.sa1[:, :], T.sa1[:, :], T.sa2[:, :], I.add), two=True)
    vec(128, ("r128", "cf1"), ("sa2",), ts(T.sa2[:, :], T.r128[:, :], c1(GC), None, I.is_equal))
    vec(128, ("sa1", "sa2"), ("sh",), tt(T.sh[:, :], T.sa1[:, :], T.sa2[:, :], I.mult), two=True)
    for qr in range(8):
        for e_ in range(2):
            o = 128 * (2 * qr + e_)
            vec(128, ("re%d" % e_, "pc"), ("bce",), ts(T.bce[:, o:o + 128], T["re%d" % e_][:, :], T.pc[:, qr:qr + 1], None, I.is_equal))
    vec(16, ("v0i",), ("v0f",), ts(T.v0f[:, :], T.v0i[:, :], HALF, None, I.subtract))
    vec(16, ("j0i",), ("j0f",), cp(T.j0f[:, :], T.j0i[:, :]))

    HE, HO, HP, HA, HJ = 0, 2 * KK, 4 * KK, 6 * KK, 16 * KK

    def v(n, lo=0, hi=None, st=1):
        w = SIZE[n]
        b = now[0]
        if n not in SCRATCH:
            n, b = "%s_%d" % (n, b), 0
        return T[n][:, b * w + lo:b * w + (w if hi is None else hi):st]

    def c2h(out, oc, src, pads, into=False, n=1):
        r = []
        for q in range(4):
            for rr in range(2):
                r.append(mm(out[32 * q:32 * q + 16, oc:oc + n * KK], pads[:, 8 * rr:8 * rr + 16], v(src, 2 * q + rr, n * W, 8),
                            not into and rr == 0, not into and rr == 1))
        return r

    def h2l(out, oc, srcs, n):
        r = [(T["pm%d" % k], v(s, k, n * KK, 2)) for s in srcs for k in range(2)]
        return [mm(out[:, oc:oc + n * ML], m[:, :], s, i == 0, i == len(r) - 1) for i, (m, s) in enumerate(r)]

    def tools(b):
        now[0] = b
        return ([T["%s_%d" % (n, b)] for n in ("PS", "PC", "PH", "PL")], (lambda n: n + str(b)), [("P", n, b) for n in "SCHL"])

    late = {}

    def again(b, y, ykey):
        (S, C, H, L), K, (PS, PC, PH, PL) = tools(b)
        pe(8 * 16, (ykey, "hp"), (PH,), c2h(H, HA, y, T.hp))
        vec(KK, (PH,), (K("ai"),), cp(v("ai"), H[:, HA:HA + KK]))
        vec(KK, (K("ai"),), (K("aj"),), ts(v("aj"), v("ai"), V - 1, None, I.bitwise_and))
        vec(KK, (K("aj"),), (K("ag"),), ts(v("ag"), v("aj"), HALF, None, I.subtract))

    def blockdiag(b):
        _, K, _ = tools(b)
        for q in range(8):
            o, i, s = v("cd", q, 16 * W, 16), v("cc", 0, W), T.mk[:, q:q + 1]
            acv(W, (K("cc0"), "mk", K("cd")), (K("cd_%d_" % q),), act(o, i, F.Copy, 0.0, s), ts(o, i, s, None, I.mult), half=True)

    def start(b):
        (S, C, H, L), K, (PS, PC, PH, PL) = tools(b)
        s = slice(b * ML, (b + 1) * ML)
        vec(7 * KK, (), (PH,), fill(H[:, 0:7 * KK], 0.0))
        vec(ML, ("v0i",), (K("lv"),), cp(v("lv"), T.v0i[:, s]))
        pe(128, ("j0f", "vi0", "vi1"), (PS,), [mm(S[:, HJ + k:HJ + KK:2], T["vi%d" % k][:, :], T.j0f[:, s], True, True) for k in range(2)])
        pe(128, ("v0f", "vi0", "vi1"), (PC,), [mm(C[:, k:KK:2], T["vi%d" % k][:, :], T.v0f[:, s], True, True) for k in range(2)])
        vec(KK, (PS,), (K("jb"),), cp(v("jb"), S[:, HJ:HJ + KK]))
        for k in range(2):
            vec(KK, (PC,), (K("vv"),), cp(v("vv", k * KK, (k + 1) * KK), C[:, 0:KK]))
        vec(2 * KK, (), (K("te"),), fill(v("te"), 0.0))
        for k in range(2):
            vec(W, ("c0s",), (K("cc%d" % k),), cp(v("cc", k * W, (k + 1) * W), v("c0s")), half=True)
        blockdiag(b)
        late[b] = ("y0s", "y0s")

    def came(b):
        _, K, _ = tools(b)
        acv(W, ("iw", K("lu")), (K("uc"),), act(v("uc"), T.iw[:, :].indirect(v("lu"))), gat=True)
        vec(W, WF + (K("lv"), K("uc")), (K("eq"),), tt(v("eq"), T.wf[:, :].indirect(v("lv")), v("uc"), I.is_equal), gat=True)

    def step(b, first):
        (S, C, H, L), K, (PS, PC, PH, PL) = tools(b)
        pe(8 * 64, ("bc", K("jb")), (PC,), [mm(C[:, 2 * W + qr:3 * W:8], T.bc[:, 128 * qr:128 * qr + 128], v("jb"), True, True) for qr in range(8)])
        vec(W, (PC, "cf7"), (K("mb"),), ts(v("mb"), C[:, 2 * W:3 * W], c1(CODE1), None, I.is_equal))
        pe(W, (K("mb"), "idb"), (PC,), [mm(C[:, 0:W], T.idb[:, :], v("mb"), True, first)])
        vr = T.wf[:, :].indirect(v("lv"))
        if not first:
            came(b)
            pe(W, (K("eq"), "sh"), (PC,), [mm(C[:, 0:W], T.sh[:, :], v("eq"), False, True)])
        acv(W, WF + (K("lv"),), (K("av"),), act(v("av"), vr), cp(v("av"), vr), gat=True)
        vec(W, (PC, K("av")), (K("pr1"),), tt(v("pr1"), v("av"), C[:, 0:W], I.mult))
        J = S[:, HJ:HJ + KK]
        if not first:
            pe(128 + 8 * 16, (K("eq"), "jp", "idb", "zb", K("jb")), (PS,),
               [mm(J, T.zb[:, :], v("jb"), True, False)] + c2h(S, HJ, "eq", T.jp, True) + [mm(J, T.idb[:, :], v("jb"), False, True)])
        vec(KK, (PS,), (K("bk"),), ts(v("bk"), J, 8.0, None, I.is_ge))
        vec(KK, (K("bk"), K("vv")), (K("te"),), tt(v("te", 0, KK), v("bk"), v("vv", 0, KK), I.mult))
        pe(16 * 16, (K("pr1"), "ep0", "ep1"), (PH,), c2h(H, HE, "pr1", T.ep0) + c2h(H, HE + KK, "pr1", T.ep1))
        vec(2 * KK, (PH, K("te")), (K("eh"),), tt(v("eh"), H[:, HE:HE + 2 * KK], v("te"), I.add))
        pe(128, (K("eh"), "pm0", "pm1"), (PL,), h2l(L, 0, ["eh"], 2))
        vec(2 * ML, (PL,), (K("le"),), ts(v("le"), L[:, 0:2 * ML], HALF, None, I.add))
        vec(KK, (PS,), (K("ok0"),), ts(v("ok", 0, KK), J, 8.0, None, I.is_lt))
        vec(KK, (PS,), (K("ok1"),), ts(v("ok", KK, 2 * KK), J, 7.0, None, I.is_lt))
        vec(KK, (PS,), (K("j2"),), ts(v("j2"), J, 2.0, None, I.add))
        w1, w2 = T.wf[:, :].indirect(v("le", 0, ML)), T.wf[:, :].indirect(v("le", ML, 2 * ML))
        acv(W, WF + (K("le"), "cf4", "cf5"), (K("zz"),), act(v("zz"), w1, F.Identity, c1(S2), c1(S1)), ts(v("zz"), w1, c1(S1), c1(S2), I.mult, I.add), gat=True)
        vec(W, WF + (K("le"), K("zz")), (K("bb"),), tt(v("bb"), w2, v("zz"), I.max), gat=True)
        vec(W, (K("bb"), "cf6"), (K("lb"),), ts(v("lb"), v("bb"), c1(S3), None, I.add))
        pe(256, ("r0b", "kc"), (PS,), [mm(S[:, 0:16 * KK], T.r0b[:, :], T.kc[:, 0:16 * KK], True, False)])
        for c in range(NCH):
            o, i = v("xg", 16 * CH * c, 16 * CH * (c + 1)), T.xw[:, :].indirect(v("lb", CH * c, CH * (c + 1)))
            acv(16 * CH, ("xw", K("lb")), (K("xg%d_" % c),), act(o, i), cp(o, i), gat=True)
            if c == 0:
                vec(2 * W, ("xw", K("le"), K("cc0"), K("cc1")), (K("po"),), tt(v("po"), T.xw[:, :].indirect(v("le")), v("cc"), I.mult), gat=True)
                pe(8 * 32, (K("po"), "ow"), (PH,), c2h(H, HO, "po", T.ow, n=2))
                acv(W, (K("bb"), "cf10"), (K("bq"),), act(v("bq"), v("bb"), F.Identity, c1(S3C)), ts(v("bq"), v("bb"), c1(S3C), None, I.add))
                vec(KK, (K("j2"), K("ok0")), (K("jq"),), tt(v("jq"), v("j2"), v("ok", 0, KK), I.mult))
                vec(KK, (K("vv"), K("ok0")), (K("vk"),), tt(v("vk"), v("vv", 0, KK), v("ok", 0, KK), I.mult))
            fns = []
            for la in range(CH * c, CH * (c + 1)):
                q, rr, k = (la % 8) // 2, la % 2, la // 8
                lo = 16 * la - 8 * rr
                fns.append(mm(S[32 * q:32 * q + 16, 16 * k:16 * k + 16], v("cd", lo, lo + 16), v("xg", 16 * la, 16 * la + 16), False, False))
            if c == NCH - 1:
                fns.append(mm(S[:, 15:16 * KK:16], T.zb[:, :], T.kc[:, 0:KK], False, True))
            pe(16 * CH, (K("xg%d_" % c), K("cd"), "zb", "kc") + tuple(K("cd_%d_" % q) for q in range(8)), (PS,), fns)
        for e_ in range(2):
            vec(8 * KK, (PS, "rs"), (K("sc%d_" % e_),), scan(v("sc", 8 * KK * e_, 8 * KK * (e_ + 1)), T.rs[:, 0:8 * KK], S[:, e_:16 * KK:2]))
        top = v("sc", 7, 16 * KK, 8)
        vec(2 * KK, (K("sc0_"), K("sc1_")), (K("ri"),), cp(v("ri"), top))
        vec(2 * KK, (K("ri"), K("sc0_"), K("sc1_")), (K("rb"),), tt(v("rb"), top, v("ri"), I.subtract))
        fns = []
        for qr in range(8):
            for e_ in range(2):
                o = 128 * (2 * qr + e_)
                fns.append(mm(C[:, W + qr:2 * W:8], T.bce[:, o:o + 128], v("rb", e_ * KK, (e_ + 1) * KK), e_ == 0, e_ == 1))
        pe(1024, (K("rb"), "bce"), (PC,), fns)
        vec(2 * KK, (K("ri"), PH), (K("gt"),), tt(v("gt"), v("ri"), H[:, HO:HO + 2 * KK], I.is_gt))
        if b in late:
            again(b, *late.pop(b))
        vec(W, (PC, "cf8"), (PC, K("m2")), ts(C[:, W:2 * W], C[:, W:2 * W], c1(CODE2), None, I.is_equal))
        vec(W, (PC, K("bq"), K("m2")), (K("pr2"),), tt(v("pr2"), v("bq"), C[:, W:2 * W], I.mult))
        vec(KK, (K("gt"), K("bk")), (K("up"),), tt(v("up"), v("gt", 0, KK), v("bk"), I.mult))
        vec(KK, (K("up"),), (K("nu"),), ts(v("nu"), v("up"), -2 * HALF, HALF, I.mult, I.add))
        vec(KK, (K("nu"), K("vv")), (K("un"),), tt(v("un"), v("nu"), v("vv", 0, KK), I.max))
        pe(128, (K("un"), "pm0", "pm1"), (PL,), h2l(L, 2 * ML, ["un"], 1))
        pe(16 * 16, (K("pr2"), "ep0", "ep1"), (PH,), c2h(H, HP, "pr2", T.ep0) + c2h(H, HP + KK, "pr2", T.ep1))
        vec(2 * KK, (K("gt"), K("ok0"), K("ok1")), (K("gk"),), tt(v("gk"), v("gt"), v("ok"), I.mult))
        acv(KK, (K("up"),), (K("u2"),), act(v("u2"), v("up"), F.Copy, 0.0, 32.0))
        vec(KK, (K("jq"), K("u2")), (K("jq"),), tt(v("jq"), v("jq"), v("u2"), I.add))
        vec(2 * KK, (K("gk"),), (K("ng"),), ts(v("ng"), v("gk"), -8192.0, 8192.0, I.mult, I.add))
        vec(2 * KK, (K("ng"), K("vv")), (K("vg"),), tt(v("vg"), v("ng"), v("vv"), I.add))
        vec(KK, (K("bk"), K("up")), (K("tp"),), tt(v("tp"), v("bk"), v("up"), I.subtract))
        vec(KK, (K("tp"), K("ag")), (K("at"),), tt(v("at"), v("tp"), v("ag"), I.mult))
        vec(ML, (PL,), (K("lu"),), ts(v("lu"), L[:, 2 * ML:3 * ML], HALF, None, I.add))
        P2 = H[:, HP:HP + 2 * KK]
        vec(2 * KK, (PH, K("vg")), (K("nn"),), tt(v("nn"), P2, v("vg"), I.not_equal))
        vec(2 * KK, (PH, K("vg")), (K("hh"),), tt(v("hh"), P2, v("vg"), I.is_equal))
        vec(KK, (PH, K("up")), (K("pu"),), tt(v("pu"), H[:, HP:HP + KK], v("up"), I.mult))
        vec(KK, (K("hh"), K("nn")), (K("g2"),), tt(v("g2"), v("hh", KK, 2 * KK), v("nn", 0, KK), I.mult))
        vec(KK, (K("vk"), K("nn")), (K("vy"),), tt(v("vy"), v("vk"), v("nn", 0, KK), I.mult))
        vec(KK, (K("hh"), K("eh")), (K("a1"),), tt(v("a1"), v("hh", 0, KK), v("eh", 0, KK), I.mult))
        vec(KK, (K("at"), K("pu")), (K("s1"),), tt(v("s1"), v("at"), v("pu"), I.add))
        vec(KK, (K("jq"), K("nn")), (K("jq"),), tt(v("jq"), v("jq"), v("nn", 0, KK), I.mult))
        vec(KK, (K("g2"), K("eh")), (K("a2"),), tt(v("a2"), v("g2"), v("eh", KK, 2 * KK), I.mult))
        vec(KK, (K("vy"), K("nn")), (K("yy"),), tt(v("yy"), v("vy"), v("nn", KK, 2 * KK), I.mult))
        vec(KK, (K("s1"), K("a1")), (K("s2"),), tt(v("s2"), v("s1"), v("a1"), I.add))
        pe(64 * 6, (K("s2"), K("a2"), K("yy"), "pm0", "pm1"), (PL,), h2l(L, 3 * ML, ["s2", "a2", "yy"], 1))
        vec(ML, (PL,), (K("lv"),), ts(v("lv"), L[:, 3 * ML:4 * ML], HALF, None, I.add))
        vec(KK, (K("jq"), K("nn")), (K("jb"),), tt(v("jb"), v("jq"), v("nn", KK, 2 * KK), I.mult))
        vec(KK, (K("a2"), K("yy")), (K("vt"),), tt(v("vt"), v("a2"), v("yy"), I.add))
        for k in range(2):
            vec(KK, (K("vt"), K("s2")), (K("vv"),), tt(v("vv", k * KK, (k + 1) * KK), v("vt"), v("s2"), I.add))

    def change(b, t):
        _, K, _ = tools(b)
        xn, yn = "xv%d" % t, "yv%d" % t
        xk, yk = K(xn + "_"), K(yn + "_")
        xv, yv, sem = v(xn), v(yn), "ar_%d_%d" % (b, t)
        i = T.xw[:, :].indirect(v("lv"))
        acv(W, ("xw", K("lv")), (xk,), act(xv, i), cp(xv, i), gat=True)
        msk = sum(1 << e for e in engines_of(topo, core, nxt))
        rid, pid = topo.addr(nxt)[:2]
        op("G", 0.5, (xk,), (), [lambda e: e.remote_dma(yv, xv, T.sem[sem], T.sem.sent, pid, rid, msk)], "remote")
        op("N", 0.0, (xk,), (yk,), [], sem, len(engines_of(topo, prv, core)), 3.5)
        vec(W, (xk, yk), (K("dy"),), tt(v("dy"), yv, xv, I.subtract), two=True)
        acv(W, (K("dy"),), (K("dy"),), act(v("dy"), v("dy"), F.Sign))
        vec(W, (K("dy"), K("cc0")), (K("cn"),), tt(v("cn"), v("cc", 0, W), v("dy"), I.add), two=True)
        if t == NCHG - 1:
            vec(W, (K("cn"),), (K("co"),), ts(v("co_s"), v("cn"), 15.0, -15.0, I.min, I.max))
            dma("S", T.co[:, b * W:(b + 1) * W], v("co_s"), (K("co"),), (K("out_c"),), 2.0)
            return
        for k in range(2):
            vec(W, (K("cn"),), (K("cc%d" % k),), ts(v("cc", k * W, (k + 1) * W), v("cn"), 15.0, -15.0, I.min, I.max))
        blockdiag(b)
        late[b] = (yn, yk)

    def finish(b):
        (S, C, H, L), K, (PS, PC, PH, PL) = tools(b)
        came(b)
        fns = [mm(C[:, 0:W], T.zb[:, :], T.bc[:, 0:W], True, False)]
        fns += [mm(C[:, qr:W:8], T.bc[:, 128 * qr:128 * qr + 128], v("jb"), False, False) for qr in range(8)]
        pe(W + 8 * 64, ("zb", "bc", K("jb")), (PC,), fns)
        pe(W, (K("eq"), "jwc"), (PC,), [mm(C[:, 0:W], T.jwc[:, :], v("eq"), False, True)])
        acv(W, ("iw", K("lv")), (K("vc"),), act(v("vo_s"), T.iw[:, :].indirect(v("lv")), F.Copy, HALF), gat=True)
        w = slice(b * W, (b + 1) * W)
        dma("S", T.vo[:, w], T.vo_s[0:128:16, w], (K("vc"),), (K("out_v"),), 2.0)
        acv(W, (PC,), (K("jo"),), act(v("jo_s"), C[:, 0:W]), cp(v("jo_s"), C[:, 0:W]))
        dma("S", T.jo[:, w], T.jo_s[0:128:16, w], (K("jo"),), (K("out_j"),), 2.0)

    for b in range(NB):
        start(b)
    for s in range(1, STEPS + 1):
        for b in range(NB):
            step(b, s == 1)
            if s % 2 == 0:
                change(b, s // 2 - 1)
    for b in range(NB):
        finish(b)
    return ops


def schedule(ops, keep, near, lead, noise=None):
    n = len(ops)
    succ = [[] for _ in range(n)]
    for i, o in enumerate(ops):
        for d in o["deps"] | o["soft"]:
            succ[d].append(i)
    rest = [0.0] * n
    for i in range(n - 1, -1, -1):
        rest[i] = ops[i]["cost"] + ops[i]["lat"] + WAKE + max([rest[j] for j in succ[i]], default=0.0)
    rest = [r + (lead if ops[i]["b"] == 0 else 0.0) + (noise[i] if noise else 0.0) for i, r in enumerate(rest)]
    left = [len(o["deps"] | o["soft"]) for o in ops]
    ready, both = {q: [] for q in "VAPGSN"}, []
    free = {q: 0.0 for q in "VAPGSN"}
    at, start, eng = [0.0] * n, [0.0] * n, [o["eng"] for o in ops]
    end_all = 0.0
    def push(i):
        (both if ops[i]["alt"] else ready[eng[i]]).append(i)
    for i in range(n):
        if not left[i]:
            push(i)
    for _ in range(n):
        best = None
        for q in "NPVASG":
            cand = ready[q] + (both if q in "VA" else [])
            if not cand:
                continue
            def when(i):
                return max(free[q], at[i]) + (keep if q == "V" and ops[i]["alt"] else 0.0)
            t0 = min(when(i) for i in cand) + near
            i = max((i for i in cand if when(i) <= t0), key=lambda i: (rest[i], -i))
            t = when(i)
            if best is None or t < best[0]:
                best = (t, q, i)
        t, q, i = best
        t = max(free[q], at[i])
        o = ops[i]
        (both if o["alt"] else ready[q]).remove(i)
        cost = o["cost"]
        if o["alt"]:
            eng[i] = q
            if q == "V":
                cost = o["alt"][1]
        if q != "N":
            free[q] = t + cost
        start[i] = t
        end = t + cost + o["lat"]
        end_all = max(end_all, end)
        for j in succ[i]:
            at[j] = max(at[j], end + WAKE if i in ops[j]["deps"] else t + cost)
            left[j] -= 1
            if not left[j]:
                push(j)
    return end_all, sorted(range(n), key=lambda i: (start[i], i)), eng


def emit(g, T, ops, order, eng):
    que = {"V": g.vector, "A": g.scalar, "P": g.tensor, "G": g, "S": g.sync}
    cnt = {q: 0 for q in "VAPG"}
    know = {q: {} for q in "VAPGS"}
    after, pos = {}, {i: k for k, i in enumerate(order)}
    for i in order:
        o, q = ops[i], eng[i]
        assert all(pos[d] < pos[i] for d in o["deps"] | o["soft"])
        if q == "N":
            after[i] = (o["sem"], o["val"], {o["sem"]: o["val"]})
            continue
        kn, need, src = know[q], {}, {}
        for d in o["deps"]:
            s, n, m = after[d]
            if s is not None and kn.get(s, 0) < n and need.get(s, 0) < n:
                need[s], src[s] = n, m
        for s in sorted(need):
            if not any(s2 != s and src[s2].get(s, 0) >= need[s] for s2 in need):
                que[q].wait_ge(T.sem[s], need[s])
        for s in need:
            for s2, v2 in src[s].items():
                kn[s2] = max(kn.get(s2, 0), v2)
            kn[s] = max(kn.get(s, 0), need[s])
        fns = o["alt"][2] if o["alt"] and q == "V" else o["fns"]
        m = dict(kn)
        if o["sem"] == "remote":
            fns[0](que[q])
            after[i] = (None, 0, {})
        elif o["sem"] is not None:
            fns[0](que[q])
            m[o["sem"]] = o["val"]
            after[i] = (o["sem"], o["val"], m)
        else:
            s = "s" + q
            for fn in fns:
                fn(que[q]).then_inc(T.sem[s], 1)
                cnt[q] += 1
            m[s] = cnt[q]
            after[i] = (s, cnt[q], m)
    return cnt


PLANS = {}


def plan(ops):
    if "plan" not in PLANS:
        best = min(((schedule(ops, k, n, l), (k, n, l)) for k in (0.3, 1.0, 2.0) for n in (0.02, 0.15, 0.3)
                    for l in (0.0, 2.0, 6.0, 20.0)), key=lambda p: p[0][0])
        rng, top, noise = np.random.default_rng(7), best[0], np.zeros(len(ops))
        for t in range(300):
            new = noise * 0.9 + rng.normal(0.0, 0.6, len(ops)) * (rng.random(len(ops)) < 0.2)
            p = schedule(ops, best[1][0], best[1][1], best[1][2], [float(x) for x in new])
            if p[0] < top[0]:
                top, noise = p, new
        PLANS["plan"] = top
    return PLANS["plan"]


def rank_program(g, core, T, topo):
    rank = T.rank_of(core)
    if rank is None:
        return
    ops = build(T, topo, core)
    _, order, eng = plan(ops)
    cnt = emit(g, T, ops, order, eng)
    nxt = T.cores[(rank + 1) % len(T.cores)]
    g.wait_ge(T.sem.sent, len(engines_of(topo, core, nxt)) * NB * NCHG)
    for q in "VAPG":
        g.wait_ge(T.sem["s" + q], cnt[q])
    for i in order:
        o = ops[i]
        if o["sem"] is not None and o["sem"] != "remote":
            g.wait_ge(T.sem[o["sem"]], o["val"])
